import numpy as np
import ml_dtypes


def mxq(x, axis, fmt="e4m3"):
    dtype, down = {"e4m3": (ml_dtypes.float8_e4m3fn, 7), "e5m2": (ml_dtypes.float8_e5m2, 14)}[fmt]
    v = np.moveaxis(np.asarray(x, np.float32).astype(ml_dtypes.bfloat16).astype(np.float64), axis, -1)
    blocks = v.reshape(v.shape[:-1] + (-1, 32))
    amax = np.abs(blocks).max(-1, keepdims=True)
    byte = np.maximum(np.where(amax > 0, np.frexp(amax)[1] - 1 + 127, 0) - down, 1)
    scale = np.exp2(byte - 127.0)
    codes = (blocks / scale).astype(np.float32).astype(dtype).astype(np.float64)
    return np.moveaxis((codes * scale).reshape(v.shape), -1, axis)


WIDE = False


def mx_kscale(k):
    if not WIDE:
        return np.ones(k)
    levels = np.array([10, -10, 5, -5, 0])
    if k % 512:
        return np.exp2(np.random.permutation(np.resize(levels, k // 32))).repeat(32)
    a = np.empty((k // 512, 16))
    for p in range(k // 512):
        a[p, :8] = np.random.permutation(np.resize(levels, 8))
        for g in range(8):
            far = levels[np.abs(levels - a[p, g]) >= 10]
            a[p, g + 8] = far[np.random.randint(len(far))]
    return np.exp2(a.ravel()).repeat(32)


def f64(x):
    return np.asarray(x).astype(np.float64)


def striped(idx):
    return np.tile(idx.reshape(-1, 16).T, (8, 1)).astype(np.uint16)


def unstriped(offs):
    return offs[:16].T.reshape(-1).astype(np.int64)


E2M1 = np.array([0.0, 0.5, 1.0, 1.5, 2.0, 3.0, 4.0, 6.0, -0.0, -0.5, -1.0, -1.5, -2.0, -3.0, -4.0, -6.0])


def pack_weight(w, fmt):
    k, n = w.shape
    w = f64(np.asarray(w, np.float32).astype(ml_dtypes.bfloat16)).reshape(k // 32, 32, n)
    amax = np.abs(w).max(1)
    if fmt == "e4m3":
        byte = np.frexp(amax)[1] - 1 + 127 - 7
    else:
        mant, ex = np.frexp(amax / 6.0)
        byte = np.where(mant > 0.5, ex, ex - 1) + 127
    byte = np.clip(np.where(amax > 0, byte, 1), 1, 254)
    scaled = (w * np.exp2(127.0 - byte)[:, None, :]).reshape(k, n).astype(np.float32)
    by_word = np.ascontiguousarray(scaled.reshape(k // 512, 128, 4, n).transpose(0, 1, 3, 2))
    if fmt == "e4m3":
        words = by_word.astype(ml_dtypes.float8_e4m3fn).view(np.uint8)
    else:
        c = by_word.astype(ml_dtypes.float4_e2m1fn).view(np.uint8) & 0xF
        words = (c[..., 0::2] | (c[..., 1::2] << 4)).reshape(k // 512, 128, 2 * n)
    return np.ascontiguousarray(words), np.ascontiguousarray(byte.astype(np.uint8).reshape(k // 512, 16, n))


def unpack_weight(words, scales, fmt):
    g, _, n = scales.shape
    words = np.ascontiguousarray(words).reshape(g, 128, n, -1)
    if fmt == "e4m3":
        vals = words.view(ml_dtypes.float8_e4m3fn).astype(np.float64)
    else:
        nib = np.empty((g, 128, n, 4), np.uint8)
        nib[..., 0::2] = words & 0xF
        nib[..., 1::2] = words >> 4
        vals = E2M1[nib]
    vals = vals * np.repeat(np.exp2(scales.astype(np.float64) - 127.0), 8, axis=1)[..., None]
    return vals.transpose(0, 1, 3, 2).reshape(g * 512, n)


K, T, E, C, H, N = 256, 1024, 8, 128, 512, 1024


def by_expert(wq, xq):
    return np.concatenate([wq[e].T @ xq[:, e * C:(e + 1) * C] for e in range(E)], axis=1)


def setup_inputs():
    n = np.random.standard_normal
    v = mx_kscale(N)
    u = mx_kscale(H)
    slot_token = np.random.permutation(T)[:E * C]
    w_slot = np.random.uniform(0.2, 1.0, E * C)
    partner = np.random.permutation(T)[:E * C]
    dy = pack_weight(n((N, T)) * v[:, None], "e4m3")
    wpt = [pack_weight(m, "e2m1") for m in n((E, H, K)) / np.sqrt(H) / u[None, :, None]]
    return {
        "dy_words": dy[0],
        "dy_scales": dy[1],
        "w2t": (n((E, N, H)) / np.sqrt(N) / v[None, :, None] * u).astype(np.float32),
        "w1t": (n((E, H, K)) / np.sqrt(H) / u[None, :, None]).astype(np.float32),
        "wpt_words": np.stack([m[0] for m in wpt]),
        "wpt_scales": np.stack([m[1] for m in wpt]),
        "gate": (np.tile(w_slot, (128, 1))).astype(np.float32),
        "offs": striped(slot_token),
        "offs2": striped(partner),
    }


def reference(dy_words, dy_scales, w2t, w1t, wpt_words, wpt_scales, gate, offs, offs2):
    w2tq = mxq(f64(w2t), 1, "e4m3")
    w1tq = mxq(f64(w1t), 1, "e4m3")
    wpt = np.stack([unpack_weight(wpt_words[e], wpt_scales[e], "e2m1") for e in range(E)])
    idx, idx2 = unstriped(offs), unstriped(offs2)
    gq = unpack_weight(dy_words, dy_scales, "e4m3")[:, idx]
    dh = f64(gate[:1]) * by_expert(w2tq, gq)
    dq = mxq(dh, 0, "e4m3")
    out = np.zeros((K, T))
    out[:, idx] = by_expert(w1tq, dq)
    out[:, idx2] += by_expert(wpt, dq)
    return out

@@ -1,0 +1,206 @@
+from contextlib import ExitStack
+
+import concourse.mybir as mybir
+from concourse.masks import make_identity
+
+K, T, E, C, H, N = 256, 1024, 8, 128, 512, 1024
+FLOPS = 2 * E * C * (N * H + 2 * H * K)
+
+F32 = mybir.dt.float32
+BF16 = mybir.dt.bfloat16
+I32 = mybir.dt.int32
+U32 = mybir.dt.uint32
+U16 = mybir.dt.uint16
+U8 = mybir.dt.uint8
+FP8X4 = mybir.dt.float8_e4m3fn_x4
+FP4X4 = mybir.dt.float4_e2m1fn_x4
+COPY = mybir.ActivationFunctionType.Copy
+ADD = mybir.AluOpType.add
+
+P = 128
+PACK = 4
+PASS = P * PACK
+PASSES = N // PASS
+HALVES = K // P
+GATHER_CUTS = [0, 256, 512, 1024]
+
+
+def interleave(copy, grouped, raw):
+    copy(
+        out=grouped.rearrange("p (c i) t -> p c t i", i=4),
+        in_=raw.rearrange("p t (c i) -> p c t i", i=4),
+    )
+
+
+def tile_moe_dub_none_kernel(tc, dy_words, dy_scales, w2t, w1t, wpt_words, wpt_scales, gate, offs, offs2, out):
+    nc = tc.nc
+    with ExitStack() as ctx:
+        keep = ctx.enter_context(tc.tile_pool(name="keep", bufs=1))
+        raw2_pool = ctx.enter_context(tc.tile_pool(name="raw2", bufs=11))
+        raw1_pool = ctx.enter_context(tc.tile_pool(name="raw1", bufs=8))
+        work = ctx.enter_context(tc.tile_pool(name="work", bufs=4))
+        psum = ctx.enter_context(tc.psum_pool(name="psum", bufs=2))
+
+        token_list = keep.tile([P, T // 16], U16, name="token_list")
+        partner_list = keep.tile([P, T // 16], U16, name="partner_list")
+        dy_win = [keep.tile([P, T], I32, name="dy_win%d" % s, align_bytes=64) for s in range(PASSES)]
+        dys_win = keep.tile([P, T], U8, name="dys_win", align_bytes=64)
+        g_words = [keep.tile([P, T], U32, name="g_words%d" % s, align_bytes=64) for s in range(PASSES)]
+        g_scales = keep.tile([P, T], U8, name="g_scales", align_bytes=64)
+        wp_words = keep.tile([P, E, 2 * K], U8, name="wp_words", align_bytes=64)
+        wp_scales = keep.tile([P, E, K], U8, name="wp_scales", align_bytes=64)
+        gate_rows = keep.tile([P, C], F32, name="gate_rows")
+        gate_cols = keep.tile([P, E], F32, name="gate_cols")
+        ident = keep.tile([P, P], F32, name="ident")
+        dx_slots = keep.tile([P, HALVES, E * C], F32, name="dx_slots")
+        dp_slots = keep.tile([P, HALVES, E * C], F32, name="dp_slots")
+        dx_win = [keep.tile([P, T], F32, name="dx_win%d" % h) for h in range(HALVES)]
+        dp_win = [keep.tile([P, T], F32, name="dp_win%d" % h) for h in range(HALVES)]
+
+        nc.vector.memset(dys_win[:].bitcast(I32), 0)
+        nc.vector.memset(wp_scales[:].rearrange("p e k -> p (e k)").bitcast(I32), 0)
+        make_identity(nc, ident[:])
+
+        raw2 = {}
+        raw1 = {}
+
+        def load_w2(e, s):
+            raw2[e, s] = raw2_pool.tile([P, PACK, H], F32, name="raw2")
+            nc.sync.dma_start(out=raw2[e, s][:], in_=w2t[e, s * PASS : (s + 1) * PASS, :].rearrange("(p j) i -> p j i", j=PACK))
+
+        def load_w1(e):
+            raw1[e] = raw1_pool.tile([P, PACK, K], F32, name="raw1")
+            nc.sync.dma_start(out=raw1[e][:], in_=w1t[e].rearrange("(p j) k -> p j k", j=PACK))
+
+        def load_dy(s):
+            nc.sync.dma_start(out=dy_win[s][:], in_=dy_words[s].rearrange("p t d -> p (t d)").bitcast(I32))
+
+        def load_wp(e0, e1):
+            nc.sync.dma_start(
+                out=wp_words[:, e0:e1, :].bitcast(I32),
+                in_=wpt_words[e0:e1, 0].rearrange("e p b -> p e b").bitcast(I32),
+            )
+
+        nc.sync.dma_start(token_list[:], offs)
+        load_dy(0)
+        load_w2(0, 0)
+        load_dy(1)
+        load_w2(0, 1)
+        for q in range(4):
+            nc.sync.dma_start(
+                out=dys_win[32 * q : 32 * q + 4 * PASSES, :].bitcast(I32),
+                in_=dy_scales[:, 4 * q : 4 * q + 4, :].bitcast(I32),
+            )
+        nc.sync.dma_start(out=gate_rows[:], in_=gate.rearrange("p (e u) -> (p e) u", u=C)[0:P, :])
+        load_w1(0)
+        load_w2(1, 0)
+        load_wp(0, 2)
+        for q in range(4):
+            nc.sync.dma_start(
+                out=wp_scales[32 * q : 32 * q + 4, :, :].bitcast(I32),
+                in_=wpt_scales[:, 0, 4 * q : 4 * q + 4, :].rearrange("e r k -> r e k").bitcast(I32),
+            )
+        load_w2(1, 1)
+        nc.sync.dma_start(partner_list[:], offs2)
+        load_w1(1)
+        load_wp(2, E)
+        for e in range(2, E):
+            load_w2(e, 0)
+            load_w2(e, 1)
+            load_w1(e)
+
+        gate_t = psum.tile([P, 2, P], F32, name="turned")
+        nc.tensor.transpose(gate_t[:, 0, :], gate_rows[:], ident[:])
+        nc.scalar.activation(out=gate_cols[:], in_=gate_t[:, 0, 0:E], func=COPY)
+
+        def gather(a, b):
+            picks = token_list[:, a // 16 : b // 16]
+            for s in range(PASSES):
+                nc.vector.tensor_copy(g_words[s][:, a:b], dy_win[s][:].bitcast(U32).indirect(picks))
+            nc.vector.tensor_copy(g_scales[:, a:b], dys_win[:].indirect(picks))
+
+        for e in range(E):
+            slots = slice(e * C, (e + 1) * C)
+            if e * C in GATHER_CUTS:
+                gather(e * C, GATHER_CUTS[GATHER_CUTS.index(e * C) + 1])
+            acc = psum.tile([P, H], F32, name="acc")
+            for s in range(PASSES):
+                grp2 = work.tile([P, H, PACK], BF16, name="grp2", align_bytes=64)
+                interleave(nc.scalar.copy, grp2[:], raw2[e, s][:])
+                w2c = work.tile([P, H], U32, name="w2c", align_bytes=64)
+                w2s = work.tile([P, H], U8, name="w2s", align_bytes=64)
+                nc.vector.quantize_mx(out=w2c[:].bitcast(FP8X4), scales=w2s[:], in_=grp2[:].rearrange("p i t -> p (i t)"))
+                nc.tensor.matmul_mx(
+                    out=acc[:],
+                    lhsT=g_words[s][:, slots].bitcast(FP8X4),
+                    lhsT_scale=g_scales[4 * s : P, slots],
+                    rhs=w2c[:].bitcast(FP8X4),
+                    rhs_scale=w2s[:],
+                    start=(s == 0),
+                    stop=(s == PASSES - 1),
+                )
+            dh = work.tile([P, H], BF16, name="dh", align_bytes=64)
+            nc.scalar.activation(
+                out=dh[:].rearrange("j (u p d) -> j u p d", u=2, d=2),
+                in_=acc[:].rearrange("j (p u d) -> j u p d", u=2, d=2),
+                func=COPY,
+                scale=gate_cols[:, e : e + 1],
+            )
+            turned = psum.tile([P, 2, P], F32, name="turned")
+            for u in range(2):
+                nc.tensor.transpose(turned[:, u, :], dh[:].bitcast(F32)[:, u * P : (u + 1) * P], ident[:])
+            dh_t = work.tile([P, C * PACK], BF16, name="dh_t", align_bytes=64)
+            nc.scalar.copy(
+                out=dh_t[:].bitcast(F32).rearrange("p (j u) -> p j u", u=2),
+                in_=turned[:].rearrange("p u j -> p j u"),
+            )
+            dqc = work.tile([P, C], U32, name="dqc", align_bytes=64)
+            dqs = work.tile([P, C], U8, name="dqs", align_bytes=64)
+            nc.vector.quantize_mx(out=dqc[:].bitcast(FP8X4), scales=dqs[:], in_=dh_t[:])
+
+            dp_ps = psum.tile([P, HALVES, C], F32, name="dp_ps")
+            for h in range(HALVES):
+                nc.tensor.matmul_mx(
+                    out=dp_ps[:, h, :],
+                    lhsT=wp_words[:, e, 2 * P * h : 2 * P * (h + 1)].bitcast(FP4X4),
+                    lhsT_scale=wp_scales[:, e, P * h : P * (h + 1)],
+                    rhs=dqc[:].bitcast(FP8X4),
+                    rhs_scale=dqs[:],
+                    start=True,
+                    stop=True,
+                )
+            nc.scalar.copy(out=dp_slots[:, :, slots], in_=dp_ps[:])
+
+            grp1 = work.tile([P, K, PACK], BF16, name="grp1", align_bytes=64)
+            interleave(nc.vector.tensor_copy, grp1[:], raw1[e][:])
+            w1c = work.tile([P, K], U32, name="w1c", align_bytes=64)
+            w1s = work.tile([P, K], U8, name="w1s", align_bytes=64)
+            nc.vector.quantize_mx(out=w1c[:].bitcast(FP8X4), scales=w1s[:], in_=grp1[:].rearrange("p k t -> p (k t)"))
+            dx_ps = psum.tile([P, HALVES, C], F32, name="dx_ps")
+            for h in range(HALVES):
+                nc.tensor.matmul_mx(
+                    out=dx_ps[:, h, :],
+                    lhsT=w1c[:, P * h : P * (h + 1)].bitcast(FP8X4),
+                    lhsT_scale=w1s[:, P * h : P * (h + 1)],
+                    rhs=dqc[:].bitcast(FP8X4),
+                    rhs_scale=dqs[:],
+                    start=True,
+                    stop=True,
+                )
+            nc.scalar.copy(out=dx_slots[:, :, slots], in_=dx_ps[:])
+
+        def scatter(e, h):
+            slots = slice(e * C, (e + 1) * C)
+            cols = slice(e * C // 16, (e + 1) * C // 16)
+            nc.vector.tensor_copy(dp_win[h][:].indirect(partner_list[:, cols]), dp_slots[:, h, slots])
+            nc.vector.tensor_copy(dx_win[h][:].indirect(token_list[:, cols]), dx_slots[:, h, slots])
+
+        for e in range(E - 1):
+            for h in range(HALVES):
+                scatter(e, h)
+        for h in range(HALVES):
+            scatter(E - 1, h)
+            for c0 in range(0, T, 512):
+                total = work.tile([P, 512], F32, name="total")
+                nc.vector.tensor_tensor(total[:], dx_win[h][:, c0 : c0 + 512], dp_win[h][:, c0 : c0 + 512], ADD)
+                nc.sync.dma_start(out=out[h * P : (h + 1) * P, c0 : c0 + 512], in_=total[:])

@@ -22,7 +22,14 @@ PACK = 4
 PASS = P * PACK
 PASSES = N // PASS
 HALVES = K // P
-GATHER_CUTS = [0, 256, 512, 1024]
+QUADRANTS = 4
+LIST_STEP = 16
+HALF_H = H // 2
+GATHER_CUTS = (0, 2 * C, E * C)
+FIRST_LATE_W1 = E - 2
+ADD_COLUMNS = 512
+RAW_W2_BUFS = 11
+WORK_BUFS = 4
 
 
 def interleave(copy, grouped, raw):
@@ -32,175 +39,250 @@ def interleave(copy, grouped, raw):
     )
 
 
-def tile_moe_dub_none_kernel(tc, dy_words, dy_scales, w2t, w1t, wpt_words, wpt_scales, gate, offs, offs2, out):
+def tile_moe_dub_none_kernel(
+    tc, dy_words, dy_scales, w2t, w1t, wpt_words, wpt_scales, gate, offs, offs2, out
+):
     nc = tc.nc
     with ExitStack() as ctx:
         keep = ctx.enter_context(tc.tile_pool(name="keep", bufs=1))
-        raw2_pool = ctx.enter_context(tc.tile_pool(name="raw2", bufs=11))
-        raw1_pool = ctx.enter_context(tc.tile_pool(name="raw1", bufs=8))
-        work = ctx.enter_context(tc.tile_pool(name="work", bufs=4))
+        raw2_pool = ctx.enter_context(tc.tile_pool(name="raw2", bufs=RAW_W2_BUFS))
+        raw1_pool = ctx.enter_context(tc.tile_pool(name="raw1", bufs=E))
+        work = ctx.enter_context(tc.tile_pool(name="work", bufs=WORK_BUFS))
         psum = ctx.enter_context(tc.psum_pool(name="psum", bufs=2))
 
-        token_list = keep.tile([P, T // 16], U16, name="token_list")
-        partner_list = keep.tile([P, T // 16], U16, name="partner_list")
+        piece_widths = [b - a for a, b in zip(GATHER_CUTS, GATHER_CUTS[1:])]
+        token_list = keep.tile([P, T // LIST_STEP], U16, name="token_list")
+        partner_list = keep.tile([P, T // LIST_STEP], U16, name="partner_list")
         dy_win = [keep.tile([P, T], I32, name="dy_win%d" % s, align_bytes=64) for s in range(PASSES)]
         dys_win = keep.tile([P, T], U8, name="dys_win", align_bytes=64)
-        g_words = [keep.tile([P, T], U32, name="g_words%d" % s, align_bytes=64) for s in range(PASSES)]
-        g_scales = keep.tile([P, T], U8, name="g_scales", align_bytes=64)
+        g_words = [
+            [keep.tile([P, w], U32, name="g_words%d_%d" % (s, c), align_bytes=64) for c, w in enumerate(piece_widths)]
+            for s in range(PASSES)
+        ]
+        g_scales = [keep.tile([P, w], U8, name="g_scales%d" % c, align_bytes=64) for c, w in enumerate(piece_widths)]
         wp_words = keep.tile([P, E, 2 * K], U8, name="wp_words", align_bytes=64)
         wp_scales = keep.tile([P, E, K], U8, name="wp_scales", align_bytes=64)
         gate_rows = keep.tile([P, C], F32, name="gate_rows")
         gate_cols = keep.tile([P, E], F32, name="gate_cols")
         ident = keep.tile([P, P], F32, name="ident")
-        dx_slots = keep.tile([P, HALVES, E * C], F32, name="dx_slots")
-        dp_slots = keep.tile([P, HALVES, E * C], F32, name="dp_slots")
         dx_win = [keep.tile([P, T], F32, name="dx_win%d" % h) for h in range(HALVES)]
         dp_win = [keep.tile([P, T], F32, name="dp_win%d" % h) for h in range(HALVES)]
 
-        nc.vector.memset(dys_win[:].bitcast(I32), 0)
+        nc.gpsimd.memset(dys_win[:].bitcast(I32), 0)
         nc.vector.memset(wp_scales[:].rearrange("p e k -> p (e k)").bitcast(I32), 0)
         make_identity(nc, ident[:])
 
-        raw2 = {}
-        raw1 = {}
+        raw2, raw1, grp2, grp1, w2q, w1q, acc, dh, turned, dh_t, dq, sums, staged = [{} for n in range(13)]
 
         def load_w2(e, s):
-            raw2[e, s] = raw2_pool.tile([P, PACK, H], F32, name="raw2")
-            nc.sync.dma_start(out=raw2[e, s][:], in_=w2t[e, s * PASS : (s + 1) * PASS, :].rearrange("(p j) i -> p j i", j=PACK))
+            raw2[e, s] = raw2_pool.tile([P, PACK, H], F32, name="raw2", align_bytes=64)
+            rows = w2t[e, s * PASS : (s + 1) * PASS, :]
+            nc.sync.dma_start(out=raw2[e, s][:], in_=rows.rearrange("(p j) i -> p j i", j=PACK))
 
         def load_w1(e):
-            raw1[e] = raw1_pool.tile([P, PACK, K], F32, name="raw1")
+            raw1[e] = raw1_pool.tile([P, PACK, K], F32, name="raw1", align_bytes=64)
             nc.sync.dma_start(out=raw1[e][:], in_=w1t[e].rearrange("(p j) k -> p j k", j=PACK))
 
         def load_dy(s):
             nc.sync.dma_start(out=dy_win[s][:], in_=dy_words[s].rearrange("p t d -> p (t d)").bitcast(I32))
 
-        def load_wp(e0, e1):
-            nc.sync.dma_start(
-                out=wp_words[:, e0:e1, :].bitcast(I32),
-                in_=wpt_words[e0:e1, 0].rearrange("e p b -> p e b").bitcast(I32),
-            )
+        def load_wp(e):
+            nc.sync.dma_start(out=wp_words[:, e, :].bitcast(I32), in_=wpt_words[e, 0].bitcast(I32))
 
         nc.sync.dma_start(token_list[:], offs)
         load_dy(0)
-        load_w2(0, 0)
-        load_dy(1)
-        load_w2(0, 1)
-        for q in range(4):
+        for q in range(QUADRANTS):
             nc.sync.dma_start(
                 out=dys_win[32 * q : 32 * q + 4 * PASSES, :].bitcast(I32),
                 in_=dy_scales[:, 4 * q : 4 * q + 4, :].bitcast(I32),
             )
+        load_w2(0, 0)
+        load_dy(1)
+        load_w2(0, 1)
         nc.sync.dma_start(out=gate_rows[:], in_=gate.rearrange("p (e u) -> (p e) u", u=C)[0:P, :])
-        load_w1(0)
-        load_w2(1, 0)
-        load_wp(0, 2)
-        for q in range(4):
-            nc.sync.dma_start(
-                out=wp_scales[32 * q : 32 * q + 4, :, :].bitcast(I32),
-                in_=wpt_scales[:, 0, 4 * q : 4 * q + 4, :].rearrange("e r k -> r e k").bitcast(I32),
-            )
-        load_w2(1, 1)
-        nc.sync.dma_start(partner_list[:], offs2)
-        load_w1(1)
-        load_wp(2, E)
-        for e in range(2, E):
-            load_w2(e, 0)
-            load_w2(e, 1)
-            load_w1(e)
-
-        gate_t = psum.tile([P, 2, P], F32, name="turned")
-        nc.tensor.transpose(gate_t[:, 0, :], gate_rows[:], ident[:])
-        nc.scalar.activation(out=gate_cols[:], in_=gate_t[:, 0, 0:E], func=COPY)
-
-        def gather(a, b):
-            picks = token_list[:, a // 16 : b // 16]
-            for s in range(PASSES):
-                nc.vector.tensor_copy(g_words[s][:, a:b], dy_win[s][:].bitcast(U32).indirect(picks))
-            nc.vector.tensor_copy(g_scales[:, a:b], dys_win[:].indirect(picks))
-
         for e in range(E):
-            slots = slice(e * C, (e + 1) * C)
-            if e * C in GATHER_CUTS:
-                gather(e * C, GATHER_CUTS[GATHER_CUTS.index(e * C) + 1])
-            acc = psum.tile([P, H], F32, name="acc")
+            if e + 1 < E:
+                load_w2(e + 1, 0)
+            if e < FIRST_LATE_W1:
+                load_w1(e)
+            if e + 1 < E:
+                load_w2(e + 1, 1)
+            if e >= FIRST_LATE_W1:
+                load_w1(e)
+            load_wp(e)
+            if e == 0:
+                for q in range(QUADRANTS):
+                    nc.sync.dma_start(
+                        out=wp_scales[32 * q : 32 * q + 4, :, :].bitcast(I32),
+                        in_=wpt_scales[:, 0, 4 * q : 4 * q + 4, :].rearrange("e r k -> r e k").bitcast(I32),
+                    )
+                nc.sync.dma_start(partner_list[:], offs2)
+
+        def spent(e, s, row):
+            return raw2[e, s][:, row, 0:HALF_H]
+
+        def picks(c):
+            return token_list[:, GATHER_CUTS[c] // LIST_STEP : GATHER_CUTS[c + 1] // LIST_STEP]
+
+        def gather_words(s, c):
+            nc.vector.tensor_copy(g_words[s][c][:], dy_win[s][:].bitcast(U32).indirect(picks(c)))
+
+        def gather_scales(c):
+            nc.vector.tensor_copy(g_scales[c][:], dys_win[:].indirect(picks(c)))
+
+        def round_w2(e, s, cuts):
+            grp2[e, s] = work.tile([P, H, PACK], BF16, name="grp2", align_bytes=64)
+            for c0, c1 in zip(cuts, cuts[1:]):
+                interleave(nc.scalar.copy, grp2[e, s][:, c0:c1, :], raw2[e, s][:, :, c0:c1])
+
+        def quantize(values, width, tag):
+            codes = work.tile([P, width], U32, name=tag + "_codes", align_bytes=64)
+            scales = work.tile([P, width], U8, name=tag + "_scales", align_bytes=64)
+            nc.vector.quantize_mx(out=codes[:].bitcast(FP8X4), scales=scales[:], in_=values)
+            return codes, scales
+
+        def quantize_w2(e, s):
+            w2q[e, s] = quantize(grp2[e, s][:].rearrange("p i t -> p (i t)"), H, "w2")
+
+        def first_product(e):
+            acc[e] = psum.tile([P, H], F32, name="acc")
+            c = 0 if e * C < GATHER_CUTS[1] else 1
+            slots = slice(e * C - GATHER_CUTS[c], (e + 1) * C - GATHER_CUTS[c])
             for s in range(PASSES):
-                grp2 = work.tile([P, H, PACK], BF16, name="grp2", align_bytes=64)
-                interleave(nc.scalar.copy, grp2[:], raw2[e, s][:])
-                w2c = work.tile([P, H], U32, name="w2c", align_bytes=64)
-                w2s = work.tile([P, H], U8, name="w2s", align_bytes=64)
-                nc.vector.quantize_mx(out=w2c[:].bitcast(FP8X4), scales=w2s[:], in_=grp2[:].rearrange("p i t -> p (i t)"))
+                codes, scales = w2q[e, s]
                 nc.tensor.matmul_mx(
-                    out=acc[:],
-                    lhsT=g_words[s][:, slots].bitcast(FP8X4),
-                    lhsT_scale=g_scales[4 * s : P, slots],
-                    rhs=w2c[:].bitcast(FP8X4),
-                    rhs_scale=w2s[:],
+                    out=acc[e][:],
+                    lhsT=g_words[s][c][:, slots].bitcast(FP8X4),
+                    lhsT_scale=g_scales[c][4 * s : P, slots],
+                    rhs=codes[:].bitcast(FP8X4),
+                    rhs_scale=scales[:],
                     start=(s == 0),
                     stop=(s == PASSES - 1),
                 )
-            dh = work.tile([P, H], BF16, name="dh", align_bytes=64)
+
+        def gate_and_turn(e, home):
+            dh[e] = home
             nc.scalar.activation(
-                out=dh[:].rearrange("j (u p d) -> j u p d", u=2, d=2),
-                in_=acc[:].rearrange("j (p u d) -> j u p d", u=2, d=2),
+                out=dh[e].rearrange("j (u p d) -> j u p d", u=2, d=2),
+                in_=acc[e][:].rearrange("j (p u d) -> j u p d", u=2, d=2),
                 func=COPY,
                 scale=gate_cols[:, e : e + 1],
             )
-            turned = psum.tile([P, 2, P], F32, name="turned")
+            turned[e] = psum.tile([P, 2, P], F32, name="turned")
             for u in range(2):
-                nc.tensor.transpose(turned[:, u, :], dh[:].bitcast(F32)[:, u * P : (u + 1) * P], ident[:])
-            dh_t = work.tile([P, C * PACK], BF16, name="dh_t", align_bytes=64)
+                nc.tensor.transpose(turned[e][:, u, :], dh[e].bitcast(F32)[:, u * P : (u + 1) * P], ident[:])
+
+        def copy_turned(e, home):
+            dh_t[e] = home
             nc.scalar.copy(
-                out=dh_t[:].bitcast(F32).rearrange("p (j u) -> p j u", u=2),
-                in_=turned[:].rearrange("p u j -> p j u"),
+                out=dh_t[e].bitcast(F32).rearrange("p (j u) -> p j u", u=2),
+                in_=turned[e][:].rearrange("p u j -> p j u"),
             )
-            dqc = work.tile([P, C], U32, name="dqc", align_bytes=64)
-            dqs = work.tile([P, C], U8, name="dqs", align_bytes=64)
-            nc.vector.quantize_mx(out=dqc[:].bitcast(FP8X4), scales=dqs[:], in_=dh_t[:])
 
-            dp_ps = psum.tile([P, HALVES, C], F32, name="dp_ps")
+        def round_w1(e, copy, home):
+            grp1[e] = home
+            interleave(copy, grp1[e].rearrange("p (k t) -> p k t", t=PACK), raw1[e][:])
+
+        def second_product(e, kind):
+            sums[e, kind] = psum.tile([P, HALVES, C], F32, name="sums_" + kind)
+            dq_codes, dq_scales = dq[e]
             for h in range(HALVES):
+                cols = slice(P * h, P * (h + 1))
+                if kind == "p":
+                    codes = wp_words[:, e, 2 * P * h : 2 * P * (h + 1)].bitcast(FP4X4)
+                    scales = wp_scales[:, e, cols]
+                else:
+                    codes = w1q[e][0][:, cols].bitcast(FP8X4)
+                    scales = w1q[e][1][:, cols]
                 nc.tensor.matmul_mx(
-                    out=dp_ps[:, h, :],
-                    lhsT=wp_words[:, e, 2 * P * h : 2 * P * (h + 1)].bitcast(FP4X4),
-                    lhsT_scale=wp_scales[:, e, P * h : P * (h + 1)],
-                    rhs=dqc[:].bitcast(FP8X4),
-                    rhs_scale=dqs[:],
+                    out=sums[e, kind][:, h, :],
+                    lhsT=codes,
+                    lhsT_scale=scales,
+                    rhs=dq_codes[:].bitcast(FP8X4),
+                    rhs_scale=dq_scales[:],
                     start=True,
                     stop=True,
                 )
-            nc.scalar.copy(out=dp_slots[:, :, slots], in_=dp_ps[:])
 
-            grp1 = work.tile([P, K, PACK], BF16, name="grp1", align_bytes=64)
-            interleave(nc.vector.tensor_copy, grp1[:], raw1[e][:])
-            w1c = work.tile([P, K], U32, name="w1c", align_bytes=64)
-            w1s = work.tile([P, K], U8, name="w1s", align_bytes=64)
-            nc.vector.quantize_mx(out=w1c[:].bitcast(FP8X4), scales=w1s[:], in_=grp1[:].rearrange("p k t -> p (k t)"))
-            dx_ps = psum.tile([P, HALVES, C], F32, name="dx_ps")
-            for h in range(HALVES):
-                nc.tensor.matmul_mx(
-                    out=dx_ps[:, h, :],
-                    lhsT=w1c[:, P * h : P * (h + 1)].bitcast(FP8X4),
-                    lhsT_scale=w1s[:, P * h : P * (h + 1)],
-                    rhs=dqc[:].bitcast(FP8X4),
-                    rhs_scale=dqs[:],
-                    start=True,
-                    stop=True,
-                )
-            nc.scalar.copy(out=dx_slots[:, :, slots], in_=dx_ps[:])
+        def stage(e, kind, home):
+            staged[e, kind] = home.rearrange("p (h c) -> p h c", h=HALVES)
+            nc.scalar.copy(out=staged[e, kind], in_=sums[e, kind][:])
 
-        def scatter(e, h):
-            slots = slice(e * C, (e + 1) * C)
-            cols = slice(e * C // 16, (e + 1) * C // 16)
-            nc.vector.tensor_copy(dp_win[h][:].indirect(partner_list[:, cols]), dp_slots[:, h, slots])
-            nc.vector.tensor_copy(dx_win[h][:].indirect(token_list[:, cols]), dx_slots[:, h, slots])
+        def scatter(e, kind, h):
+            cols = slice(e * C // LIST_STEP, (e + 1) * C // LIST_STEP)
+            if kind == "p":
+                window = dp_win[h][:].indirect(partner_list[:, cols])
+            else:
+                window = dx_win[h][:].indirect(token_list[:, cols])
+            nc.vector.tensor_copy(window, staged[e, kind][:, h, :])
 
-        for e in range(E - 1):
-            for h in range(HALVES):
-                scatter(e, h)
+        def own_tile(name, dtype):
+            width = HALVES * C if dtype == F32 else H
+            fresh = work.tile([P, width], dtype, name=name, align_bytes=64)
+            return fresh[:]
+
+        gather_words(0, 0)
+        gather_scales(0)
+        gather_words(0, 1)
+        gather_words(1, 0)
+        gather_scales(1)
+        round_w2(0, 0, (0, H))
+        quantize_w2(0, 0)
+        gather_words(1, 1)
+        round_w2(0, 1, (0, H))
+        gate_t = psum.tile([P, 2, P], F32, name="turned")
+        nc.tensor.transpose(gate_t[:, 0, :], gate_rows[:], ident[:])
+        nc.scalar.activation(out=gate_cols[:], in_=gate_t[:, 0, 0:E], func=COPY)
+        quantize_w2(0, 1)
+        first_product(0)
+
+        for e in range(E):
+            nxt, prev = e + 1, e - 1
+            last = nxt == E
+            if last:
+                stage(prev, "p", own_tile("staged_p", F32))
+                gate_and_turn(e, own_tile("dh", BF16))
+                copy_turned(e, own_tile("dh_t", BF16))
+                stage(prev, "x", dh[e].bitcast(F32))
+            else:
+                round_w2(nxt, 0, (0, HALF_H, H))
+                gate_and_turn(e, spent(nxt, 0, 0).bitcast(BF16))
+                if e > 0:
+                    stage(prev, "p", spent(nxt, 0, 1))
+                round_w2(nxt, 1, (0, HALF_H, H))
+                copy_turned(e, spent(nxt, 1, 0).bitcast(BF16))
+                if e > 0:
+                    stage(prev, "x", spent(nxt, 1, 1))
+                quantize_w2(nxt, 0)
+            if e < FIRST_LATE_W1:
+                home = grp2[nxt, 0][:, 0:HALF_H, :].rearrange("p i t -> p (i t)")
+                round_w1(e, nc.vector.tensor_copy, home)
+            else:
+                round_w1(e, nc.scalar.copy, raw2[E - 1, 1][:, 2 + e - FIRST_LATE_W1, :].bitcast(BF16))
+            if e > 0:
+                for h in range(HALVES):
+                    scatter(prev, "p", h)
+            if e < FIRST_LATE_W1:
+                w1q[e] = quantize(grp1[e], K, "w1")
+            if not last:
+                quantize_w2(nxt, 1)
+                first_product(nxt)
+            dq[e] = quantize(dh_t[e], C, "dh")
+            second_product(e, "p")
+            if e >= FIRST_LATE_W1:
+                w1q[e] = quantize(grp1[e], K, "w1")
+            second_product(e, "x")
+            if e > 0:
+                for h in range(HALVES):
+                    scatter(prev, "x", h)
+
+        stage(E - 1, "p", own_tile("staged_p", F32))
+        stage(E - 1, "x", own_tile("staged_x", F32))
         for h in range(HALVES):
-            scatter(E - 1, h)
-            for c0 in range(0, T, 512):
-                total = work.tile([P, 512], F32, name="total")
-                nc.vector.tensor_tensor(total[:], dx_win[h][:, c0 : c0 + 512], dp_win[h][:, c0 : c0 + 512], ADD)
-                nc.sync.dma_start(out=out[h * P : (h + 1) * P, c0 : c0 + 512], in_=total[:])
+            scatter(E - 1, "p", h)
+            scatter(E - 1, "x", h)
+            for c0 in range(0, T, ADD_COLUMNS):
+                cols = slice(c0, c0 + ADD_COLUMNS)
+                total = work.tile([P, ADD_COLUMNS], F32, name="total")
+                nc.vector.tensor_tensor(total[:], dx_win[h][:, cols], dp_win[h][:, cols], ADD)
+                nc.sync.dma_start(out=out[h * P : (h + 1) * P, cols], in_=total[:])

@@ -69,8 +69,13 @@ def tile_moe_dub_none_kernel(
         dp_win = [keep.tile([P, T], F32, name="dp_win%d" % h) for h in range(HALVES)]
 
         nc.gpsimd.memset(dys_win[:].bitcast(I32), 0)
-        nc.vector.memset(wp_scales[:].rearrange("p e k -> p (e k)").bitcast(I32), 0)
         make_identity(nc, ident[:])
+        nc.gpsimd.memset(wp_scales[:].rearrange("p e k -> p (e k)").bitcast(I32), 0)
+        for q in range(QUADRANTS):
+            nc.gpsimd.dma_start(
+                out=wp_scales[32 * q : 32 * q + 4, :, :].bitcast(I32),
+                in_=wpt_scales[:, 0, 4 * q : 4 * q + 4, :].rearrange("e r k -> r e k").bitcast(I32),
+            )
 
         raw2, raw1, grp2, grp1, w2q, w1q, acc, dh, turned, dh_t, dq, sums, staged = [{} for n in range(13)]
 
@@ -111,11 +116,6 @@ def tile_moe_dub_none_kernel(
                 load_w1(e)
             load_wp(e)
             if e == 0:
-                for q in range(QUADRANTS):
-                    nc.sync.dma_start(
-                        out=wp_scales[32 * q : 32 * q + 4, :, :].bitcast(I32),
-                        in_=wpt_scales[:, 0, 4 * q : 4 * q + 4, :].rearrange("e r k -> r e k").bitcast(I32),
-                    )
                 nc.sync.dma_start(partner_list[:], offs2)
 
         def spent(e, s, row):

@@ -34,8 +34,8 @@ WORK_BUFS = 4
 
 def interleave(copy, grouped, raw):
     copy(
-        out=grouped.rearrange("p (c i) t -> p c t i", i=4),
-        in_=raw.rearrange("p t (c i) -> p c t i", i=4),
+        out=grouped.rearrange("p (c i) t -> p c t i", i=2),
+        in_=raw.rearrange("p t (c i) -> p c t i", i=2),
     )
 
 

@@ -16,6 +16,7 @@ FP8X4 = mybir.dt.float8_e4m3fn_x4
 FP4X4 = mybir.dt.float4_e2m1fn_x4
 COPY = mybir.ActivationFunctionType.Copy
 ADD = mybir.AluOpType.add
+MULT = mybir.AluOpType.mult
 
 P = 128
 PACK = 4
@@ -71,11 +72,6 @@ def tile_moe_dub_none_kernel(
         nc.gpsimd.memset(dys_win[:].bitcast(I32), 0)
         make_identity(nc, ident[:])
         nc.gpsimd.memset(wp_scales[:].rearrange("p e k -> p (e k)").bitcast(I32), 0)
-        for q in range(QUADRANTS):
-            nc.gpsimd.dma_start(
-                out=wp_scales[32 * q : 32 * q + 4, :, :].bitcast(I32),
-                in_=wpt_scales[:, 0, 4 * q : 4 * q + 4, :].rearrange("e r k -> r e k").bitcast(I32),
-            )
 
         raw2, raw1, grp2, grp1, w2q, w1q, acc, dh, turned, dh_t, dq, sums, staged = [{} for n in range(13)]
 
@@ -105,6 +101,11 @@ def tile_moe_dub_none_kernel(
         load_dy(1)
         load_w2(0, 1)
         nc.sync.dma_start(out=gate_rows[:], in_=gate.rearrange("p (e u) -> (p e) u", u=C)[0:P, :])
+        for q in range(QUADRANTS):
+            nc.sync.dma_start(
+                out=wp_scales[32 * q : 32 * q + 4, :, :].bitcast(I32),
+                in_=wpt_scales[:, 0, 4 * q : 4 * q + 4, :].rearrange("e r k -> r e k").bitcast(I32),
+            )
         for e in range(E):
             if e + 1 < E:
                 load_w2(e + 1, 0)
@@ -183,6 +184,12 @@ def tile_moe_dub_none_kernel(
             grp1[e] = home
             interleave(copy, grp1[e].rearrange("p (k t) -> p k t", t=PACK), raw1[e][:])
 
+        def round_w1_gpsimd(e, home):
+            grp1[e] = home
+            nc.gpsimd.tensor_scalar(
+                grp1[e].rearrange("p (k t) -> p k t", t=PACK), raw1[e][:].rearrange("p t k -> p k t"), 1.0, 0.0, MULT, ADD
+            )
+
         def second_product(e, kind):
             sums[e, kind] = psum.tile([P, HALVES, C], F32, name="sums_" + kind)
             dq_codes, dq_scales = dq[e]
@@ -256,21 +263,18 @@ def tile_moe_dub_none_kernel(
                 quantize_w2(nxt, 0)
             if e < FIRST_LATE_W1:
                 home = grp2[nxt, 0][:, 0:HALF_H, :].rearrange("p i t -> p (i t)")
-                round_w1(e, nc.vector.tensor_copy, home)
+                round_w1_gpsimd(e, home)
             else:
                 round_w1(e, nc.scalar.copy, raw2[E - 1, 1][:, 2 + e - FIRST_LATE_W1, :].bitcast(BF16))
             if e > 0:
                 for h in range(HALVES):
                     scatter(prev, "p", h)
-            if e < FIRST_LATE_W1:
-                w1q[e] = quantize(grp1[e], K, "w1")
             if not last:
                 quantize_w2(nxt, 1)
                 first_product(nxt)
             dq[e] = quantize(dh_t[e], C, "dh")
             second_product(e, "p")
-            if e >= FIRST_LATE_W1:
-                w1q[e] = quantize(grp1[e], K, "w1")
+            w1q[e] = quantize(grp1[e], K, "w1")
             second_product(e, "x")
             if e > 0:
                 for h in range(HALVES):

@@ -26,11 +26,16 @@ HALVES = K // P
 QUADRANTS = 4
 LIST_STEP = 16
 HALF_H = H // 2
+QUARTER_H = H // 4
 GATHER_CUTS = (0, 2 * C, E * C)
-FIRST_LATE_W1 = E - 2
-ADD_COLUMNS = 512
+FIRST_LATE_W1 = E - 1
+SEAM = 64
+VECTOR_CUT = 384
+GPSIMD_ADD = 288
+LAST_ADD = 384
 RAW_W2_BUFS = 11
 WORK_BUFS = 4
+GROUPED_BUFS = 3
 
 
 def interleave(copy, grouped, raw):
@@ -71,9 +76,15 @@ def tile_moe_dub_none_kernel(
 
         nc.gpsimd.memset(dys_win[:].bitcast(I32), 0)
         make_identity(nc, ident[:])
+        nc.gpsimd.memset(gate_rows[:], 0.0)
         nc.gpsimd.memset(wp_scales[:].rearrange("p e k -> p (e k)").bitcast(I32), 0)
+        for q in range(QUADRANTS):
+            nc.gpsimd.dma_start(
+                out=wp_scales[32 * q : 32 * q + 4, :, :].bitcast(I32),
+                in_=wpt_scales[:, 0, 4 * q : 4 * q + 4, :].rearrange("e r k -> r e k").bitcast(I32),
+            )
 
-        raw2, raw1, grp2, grp1, w2q, w1q, acc, dh, turned, dh_t, dq, sums, staged = [{} for n in range(13)]
+        raw2, raw1, grp2, grp1, w2q, w1q, acc, dh, bank, dh_t, dq, sums, staged = [{} for n in range(13)]
 
         def load_w2(e, s):
             raw2[e, s] = raw2_pool.tile([P, PACK, H], F32, name="raw2", align_bytes=64)
@@ -100,27 +111,16 @@ def tile_moe_dub_none_kernel(
         load_w2(0, 0)
         load_dy(1)
         load_w2(0, 1)
-        nc.sync.dma_start(out=gate_rows[:], in_=gate.rearrange("p (e u) -> (p e) u", u=C)[0:P, :])
-        for q in range(QUADRANTS):
-            nc.sync.dma_start(
-                out=wp_scales[32 * q : 32 * q + 4, :, :].bitcast(I32),
-                in_=wpt_scales[:, 0, 4 * q : 4 * q + 4, :].rearrange("e r k -> r e k").bitcast(I32),
-            )
-        for e in range(E):
-            if e + 1 < E:
-                load_w2(e + 1, 0)
-            if e < FIRST_LATE_W1:
-                load_w1(e)
-            if e + 1 < E:
-                load_w2(e + 1, 1)
-            if e >= FIRST_LATE_W1:
-                load_w1(e)
-            load_wp(e)
-            if e == 0:
+        nc.sync.dma_start(out=gate_rows[0:E, :], in_=gate.rearrange("p (e u) -> (p e) u", u=C)[0:E, :])
+        for e in range(1, E):
+            load_w2(e, 0)
+            if e == 1:
                 nc.sync.dma_start(partner_list[:], offs2)
-
-        def spent(e, s, row):
-            return raw2[e, s][:, row, 0:HALF_H]
+            load_wp(e - 1)
+            load_w1(e - 1)
+            load_w2(e, 1)
+        load_w1(E - 1)
+        load_wp(E - 1)
 
         def picks(c):
             return token_list[:, GATHER_CUTS[c] // LIST_STEP : GATHER_CUTS[c + 1] // LIST_STEP]
@@ -131,10 +131,28 @@ def tile_moe_dub_none_kernel(
         def gather_scales(c):
             nc.vector.tensor_copy(g_scales[c][:], dys_win[:].indirect(picks(c)))
 
-        def round_w2(e, s, cuts):
-            grp2[e, s] = work.tile([P, H, PACK], BF16, name="grp2", align_bytes=64)
-            for c0, c1 in zip(cuts, cuts[1:]):
-                interleave(nc.scalar.copy, grp2[e, s][:, c0:c1, :], raw2[e, s][:, :, c0:c1])
+        def open_pass(e, s):
+            if s == 0:
+                grp2[e] = work.tile([P, PASSES * H, PACK], BF16, name="grp2", align_bytes=64, bufs=GROUPED_BUFS)
+            grp2[e, s] = grp2[e][:, s * H : (s + 1) * H, :]
+            codes = work.tile([P, H], U32, name="w2_codes", align_bytes=64)
+            scales = work.tile([P, H], U8, name="w2_scales", align_bytes=64)
+            w2q[e, s] = codes, scales
+
+        def round_on_gpsimd(grouped, raw):
+            nc.gpsimd.tensor_scalar(grouped, raw.rearrange("p t c -> p c t"), 1.0, 0.0, MULT, ADD)
+
+        def round_w2(e, s, c0, c1, copy=nc.scalar.copy):
+            interleave(copy, grp2[e, s][:, c0:c1, :], raw2[e, s][:, :, c0:c1])
+
+        def quantize_w2(e, s, c0, c1):
+            codes, scales = w2q[e, s]
+            cols = slice(c0, c1)
+            nc.vector.quantize_mx(
+                out=codes[:, cols].bitcast(FP8X4),
+                scales=scales[:, cols],
+                in_=grp2[e, s][:, cols, :].rearrange("p i t -> p (i t)"),
+            )
 
         def quantize(values, width, tag):
             codes = work.tile([P, width], U32, name=tag + "_codes", align_bytes=64)
@@ -142,56 +160,48 @@ def tile_moe_dub_none_kernel(
             nc.vector.quantize_mx(out=codes[:].bitcast(FP8X4), scales=scales[:], in_=values)
             return codes, scales
 
-        def quantize_w2(e, s):
-            w2q[e, s] = quantize(grp2[e, s][:].rearrange("p i t -> p (i t)"), H, "w2")
+        def quantize_dh(e):
+            dq[e] = quantize(dh_t[e], C, "dh")
 
-        def first_product(e):
-            acc[e] = psum.tile([P, H], F32, name="acc")
+        def quantize_w1(e):
+            w1q[e] = quantize(grp1[e].rearrange("p k t -> p (k t)"), K, "w1")
+
+        def first_product(e, s, c0, c1):
+            if s == 0:
+                acc[e, c0] = psum.tile([P, c1 - c0], F32, name="acc")
             c = 0 if e * C < GATHER_CUTS[1] else 1
             slots = slice(e * C - GATHER_CUTS[c], (e + 1) * C - GATHER_CUTS[c])
-            for s in range(PASSES):
-                codes, scales = w2q[e, s]
-                nc.tensor.matmul_mx(
-                    out=acc[e][:],
-                    lhsT=g_words[s][c][:, slots].bitcast(FP8X4),
-                    lhsT_scale=g_scales[c][4 * s : P, slots],
-                    rhs=codes[:].bitcast(FP8X4),
-                    rhs_scale=scales[:],
-                    start=(s == 0),
-                    stop=(s == PASSES - 1),
-                )
+            codes, scales = w2q[e, s]
+            nc.tensor.matmul_mx(
+                out=acc[e, c0][:],
+                lhsT=g_words[s][c][:, slots].bitcast(FP8X4),
+                lhsT_scale=g_scales[c][4 * s : P, slots],
+                rhs=codes[:, c0:c1].bitcast(FP8X4),
+                rhs_scale=scales[:, c0:c1],
+                start=(s == 0),
+                stop=(s == PASSES - 1),
+            )
 
-        def gate_and_turn(e, home):
-            dh[e] = home
+        def gate_sums(e, c0, c1):
             nc.scalar.activation(
-                out=dh[e].rearrange("j (u p d) -> j u p d", u=2, d=2),
-                in_=acc[e][:].rearrange("j (p u d) -> j u p d", u=2, d=2),
+                out=dh[e][:, :, c0 // PACK : c1 // PACK].bitcast(BF16).rearrange("j u (p d) -> j u p d", d=2),
+                in_=acc[e, c0][:].rearrange("j (p u d) -> j u p d", u=2, d=2),
                 func=COPY,
                 scale=gate_cols[:, e : e + 1],
             )
-            turned[e] = psum.tile([P, 2, P], F32, name="turned")
-            for u in range(2):
-                nc.tensor.transpose(turned[e][:, u, :], dh[e].bitcast(F32)[:, u * P : (u + 1) * P], ident[:])
+
+        def turn(e):
+            for u in (1, 0):
+                nc.tensor.transpose(bank[e][:, u, :], dh[e][:, u, :], ident[:])
 
         def copy_turned(e, home):
             dh_t[e] = home
             nc.scalar.copy(
                 out=dh_t[e].bitcast(F32).rearrange("p (j u) -> p j u", u=2),
-                in_=turned[e][:].rearrange("p u j -> p j u"),
+                in_=bank[e][:, 0:2, :].rearrange("p u j -> p j u"),
             )
 
-        def round_w1(e, copy, home):
-            grp1[e] = home
-            interleave(copy, grp1[e].rearrange("p (k t) -> p k t", t=PACK), raw1[e][:])
-
-        def round_w1_gpsimd(e, home):
-            grp1[e] = home
-            nc.gpsimd.tensor_scalar(
-                grp1[e].rearrange("p (k t) -> p k t", t=PACK), raw1[e][:].rearrange("p t k -> p k t"), 1.0, 0.0, MULT, ADD
-            )
-
-        def second_product(e, kind):
-            sums[e, kind] = psum.tile([P, HALVES, C], F32, name="sums_" + kind)
+        def second_product(e, kind, homes):
             dq_codes, dq_scales = dq[e]
             for h in range(HALVES):
                 cols = slice(P * h, P * (h + 1))
@@ -202,7 +212,7 @@ def tile_moe_dub_none_kernel(
                     codes = w1q[e][0][:, cols].bitcast(FP8X4)
                     scales = w1q[e][1][:, cols]
                 nc.tensor.matmul_mx(
-                    out=sums[e, kind][:, h, :],
+                    out=homes[h],
                     lhsT=codes,
                     lhsT_scale=scales,
                     rhs=dq_codes[:].bitcast(FP8X4),
@@ -211,9 +221,12 @@ def tile_moe_dub_none_kernel(
                     stop=True,
                 )
 
-        def stage(e, kind, home):
-            staged[e, kind] = home.rearrange("p (h c) -> p h c", h=HALVES)
-            nc.scalar.copy(out=staged[e, kind], in_=sums[e, kind][:])
+        def own_bank(name):
+            fresh = psum.tile([P, 4, C], F32, name=name)
+            return fresh[:]
+
+        def stage(source, home):
+            nc.scalar.copy(out=home, in_=source)
 
         def scatter(e, kind, h):
             cols = slice(e * C // LIST_STEP, (e + 1) * C // LIST_STEP)
@@ -221,11 +234,14 @@ def tile_moe_dub_none_kernel(
                 window = dp_win[h][:].indirect(partner_list[:, cols])
             else:
                 window = dx_win[h][:].indirect(token_list[:, cols])
-            nc.vector.tensor_copy(window, staged[e, kind][:, h, :])
+            nc.vector.tensor_copy(window, staged[e, kind, h])
 
-        def own_tile(name, dtype):
-            width = HALVES * C if dtype == F32 else H
-            fresh = work.tile([P, width], dtype, name=name, align_bytes=64)
+        def scatters(e, kind):
+            for h in range(HALVES):
+                scatter(e, kind, h)
+
+        def own_tile(name, shape, dtype):
+            fresh = work.tile([P] + shape, dtype, name=name, align_bytes=64)
             return fresh[:]
 
         gather_words(0, 0)
@@ -233,60 +249,107 @@ def tile_moe_dub_none_kernel(
         gather_words(0, 1)
         gather_words(1, 0)
         gather_scales(1)
-        round_w2(0, 0, (0, H))
-        quantize_w2(0, 0)
+        open_pass(0, 0)
+        round_w2(0, 0, 0, H)
+        quantize_w2(0, 0, 0, H)
+        first_product(0, 0, 0, H)
         gather_words(1, 1)
-        round_w2(0, 1, (0, H))
-        gate_t = psum.tile([P, 2, P], F32, name="turned")
+        open_pass(0, 1)
+        round_w2(0, 1, 0, HALF_H)
+        round_w2(0, 1, HALF_H, H)
+        gate_t = own_bank("turned")
         nc.tensor.transpose(gate_t[:, 0, :], gate_rows[:], ident[:])
         nc.scalar.activation(out=gate_cols[:], in_=gate_t[:, 0, 0:E], func=COPY)
-        quantize_w2(0, 1)
-        first_product(0)
+        quantize_w2(0, 1, 0, HALF_H)
 
         for e in range(E):
             nxt, prev = e + 1, e - 1
             last = nxt == E
             if last:
-                stage(prev, "p", own_tile("staged_p", F32))
-                gate_and_turn(e, own_tile("dh", BF16))
-                copy_turned(e, own_tile("dh_t", BF16))
-                stage(prev, "x", dh[e].bitcast(F32))
+                quantize_w2(e, 1, HALF_H, VECTOR_CUT)
+                first_product(e, 1, HALF_H, H)
             else:
-                round_w2(nxt, 0, (0, HALF_H, H))
-                gate_and_turn(e, spent(nxt, 0, 0).bitcast(BF16))
-                if e > 0:
-                    stage(prev, "p", spent(nxt, 0, 1))
-                round_w2(nxt, 1, (0, HALF_H, H))
-                copy_turned(e, spent(nxt, 1, 0).bitcast(BF16))
-                if e > 0:
-                    stage(prev, "x", spent(nxt, 1, 1))
-                quantize_w2(nxt, 0)
-            if e < FIRST_LATE_W1:
-                home = grp2[nxt, 0][:, 0:HALF_H, :].rearrange("p i t -> p (i t)")
-                round_w1_gpsimd(e, home)
+                quantize_w2(e, 1, HALF_H, H)
+                first_product(e, 1, 0, H)
+            grp1[e] = grp2[e, 1][:, HALF_H:H, :]
+            if e == 0:
+                interleave(nc.vector.tensor_copy, grp1[e], raw1[e][:])
             else:
-                round_w1(e, nc.scalar.copy, raw2[E - 1, 1][:, 2 + e - FIRST_LATE_W1, :].bitcast(BF16))
+                round_on_gpsimd(grp1[e], raw1[e][:])
             if e > 0:
+                scatters(prev, "p")
+                scatter(prev, "x", 0)
+                if not last:
+                    scatter(prev, "x", 1)
+            if last:
+                gate_sums(e, HALF_H, H)
+                turn(e)
+                copy_turned(e, own_tile("dh_t", [H], BF16))
+                staged[prev, "x", 1] = own_tile("staged", [C], F32)
+                stage(bank[e][:, 2, :], staged[prev, "x", 1])
+                quantize_w1(e)
+                quantize_dh(e)
+                by_half = [own_bank("sums_p"), own_bank("sums_x")]
+                second_product(e, "p", [by_half[h][:, 0, :] for h in range(HALVES)])
+                second_product(e, "x", [by_half[h][:, 1, :] for h in range(HALVES)])
+                scatter(prev, "x", 1)
                 for h in range(HALVES):
-                    scatter(prev, "p", h)
-            if not last:
-                quantize_w2(nxt, 1)
-                first_product(nxt)
-            dq[e] = quantize(dh_t[e], C, "dh")
-            second_product(e, "p")
-            w1q[e] = quantize(grp1[e], K, "w1")
-            second_product(e, "x")
-            if e > 0:
+                    for g, kind in enumerate("px"):
+                        staged[e, kind, h] = own_tile("staged", [C], F32)
+                        stage(by_half[h][:, g, :], staged[e, kind, h])
+            else:
+                open_pass(nxt, 0)
+                open_pass(nxt, 1)
+                round_w2(nxt, 0, 0, HALF_H)
+                if e == 0:
+                    bank[e] = own_bank("turned")
+                seam = grp2[nxt][:, H - SEAM : H + SEAM, :].rearrange("p i t -> p (i t)").bitcast(F32)
+                dh[e] = seam.rearrange("j (u p) -> j u p", u=2)
+                gate_sums(e, 0, H)
+                turn(e)
+                round_w2(nxt, 0, HALF_H, H - SEAM)
+                copy_turned(e, own_tile("dh_t", [H], BF16))
+                round_w2(nxt, 0, H - SEAM, H)
+                quantize_dh(e)
+                quantize_w1(e)
+                bank[nxt] = own_bank("turned")
+                sums_p, sums_x = own_bank("sums_p"), own_bank("sums_x")
+                second_product(e, "p", [sums_p[:, h, :] for h in range(HALVES)])
+                held = nxt == E - 1
+                second_product(e, "x", [sums_x[:, 0, :], bank[nxt][:, 2, :] if held else sums_x[:, 1, :]])
+                quantize_w2(nxt, 0, 0, H)
+                if held:
+                    first_product(nxt, 0, 0, HALF_H)
+                    first_product(nxt, 0, HALF_H, H)
+                else:
+                    first_product(nxt, 0, 0, H)
+                round_w2(nxt, 1, VECTOR_CUT, H, nc.vector.tensor_copy)
+                round_w2(nxt, 1, 0, HALF_H)
+                round_w2(nxt, 1, HALF_H, VECTOR_CUT)
+                quantize_w2(nxt, 1, 0, HALF_H)
+                if held:
+                    first_product(nxt, 1, 0, HALF_H)
+                    quantize_w2(nxt, 1, VECTOR_CUT, H)
+                homes = raw2[nxt, 1][:, :, 0:C]
+                stage(sums_p[:, 0:2, :], homes[:, 0:2, :])
+                wide = 1 if held else 2
+                stage(sums_x[:, 0:wide, :], homes[:, 2 : 2 + wide, :])
                 for h in range(HALVES):
-                    scatter(prev, "x", h)
+                    staged[e, "p", h], staged[e, "x", h] = homes[:, h, :], homes[:, 2 + h, :]
+                if held:
+                    dh[nxt] = own_tile("dh", [2, P], F32)
+                    gate_sums(nxt, 0, HALF_H)
 
-        stage(E - 1, "p", own_tile("staged_p", F32))
-        stage(E - 1, "x", own_tile("staged_x", F32))
+        def add_and_store(adder, queue, h, c0, c1):
+            total = work.tile([P, c1 - c0], F32, name="total", bufs=5)
+            adder.tensor_tensor(total[:], dx_win[h][:, c0:c1], dp_win[h][:, c0:c1], ADD)
+            queue.dma_start(out=out[h * P : (h + 1) * P, c0:c1], in_=total[:])
+
         for h in range(HALVES):
             scatter(E - 1, "p", h)
             scatter(E - 1, "x", h)
-            for c0 in range(0, T, ADD_COLUMNS):
-                cols = slice(c0, c0 + ADD_COLUMNS)
-                total = work.tile([P, ADD_COLUMNS], F32, name="total")
-                nc.vector.tensor_tensor(total[:], dx_win[h][:, cols], dp_win[h][:, cols], ADD)
-                nc.sync.dma_start(out=out[h * P : (h + 1) * P, cols], in_=total[:])
+        add_and_store(nc.gpsimd, nc.scalar, 0, 0, GPSIMD_ADD)
+        add_and_store(nc.gpsimd, nc.scalar, 0, GPSIMD_ADD, 2 * GPSIMD_ADD)
+        add_and_store(nc.vector, nc.sync, 0, 2 * GPSIMD_ADD, T)
+        add_and_store(nc.vector, nc.sync, 1, 0, T - LAST_ADD)
+        add_and_store(nc.vector, nc.sync, 1, T - LAST_ADD, T)

@@ -31,8 +31,8 @@ GATHER_CUTS = (0, 2 * C, E * C)
 FIRST_LATE_W1 = E - 1
 SEAM = 64
 VECTOR_CUT = 384
-GPSIMD_ADD = 288
-LAST_ADD = 384
+GPSIMD_ADD = 256
+ADD_CUTS = (0, 384, 768, 1024)
 RAW_W2_BUFS = 11
 WORK_BUFS = 4
 GROUPED_BUFS = 3
@@ -116,8 +116,8 @@ def tile_moe_dub_none_kernel(
             load_w2(e, 0)
             if e == 1:
                 nc.sync.dma_start(partner_list[:], offs2)
-            load_wp(e - 1)
             load_w1(e - 1)
+            load_wp(e - 1)
             load_w2(e, 1)
         load_w1(E - 1)
         load_wp(E - 1)
@@ -133,7 +133,8 @@ def tile_moe_dub_none_kernel(
 
         def open_pass(e, s):
             if s == 0:
-                grp2[e] = work.tile([P, PASSES * H, PACK], BF16, name="grp2", align_bytes=64, bufs=GROUPED_BUFS)
+                both = work.tile([P, PASSES * H + SEAM, PACK], BF16, name="grp2", align_bytes=64, bufs=GROUPED_BUFS)
+                grp2[e] = both[:]
             grp2[e, s] = grp2[e][:, s * H : (s + 1) * H, :]
             codes = work.tile([P, H], U32, name="w2_codes", align_bytes=64)
             scales = work.tile([P, H], U8, name="w2_scales", align_bytes=64)
@@ -181,6 +182,10 @@ def tile_moe_dub_none_kernel(
                 start=(s == 0),
                 stop=(s == PASSES - 1),
             )
+
+        def seam_at(e, column):
+            seam = grp2[e][:, column - SEAM : column + SEAM, :].rearrange("p i t -> p (i t)").bitcast(F32)
+            return seam.rearrange("j (u p) -> j u p", u=2)
 
         def gate_sums(e, c0, c1):
             nc.scalar.activation(
@@ -275,7 +280,8 @@ def tile_moe_dub_none_kernel(
             if e == 0:
                 interleave(nc.vector.tensor_copy, grp1[e], raw1[e][:])
             else:
-                round_on_gpsimd(grp1[e], raw1[e][:])
+                wide = K - SEAM if last else K
+                round_on_gpsimd(grp1[e][:, 0:wide, :], raw1[e][:, :, 0:wide])
             if e > 0:
                 scatters(prev, "p")
                 scatter(prev, "x", 0)
@@ -285,26 +291,27 @@ def tile_moe_dub_none_kernel(
                 gate_sums(e, HALF_H, H)
                 turn(e)
                 copy_turned(e, own_tile("dh_t", [H], BF16))
+                interleave(nc.scalar.copy, grp1[e][:, K - SEAM : K, :], raw1[e][:, :, K - SEAM : K])
                 staged[prev, "x", 1] = own_tile("staged", [C], F32)
                 stage(bank[e][:, 2, :], staged[prev, "x", 1])
-                quantize_w1(e)
                 quantize_dh(e)
-                by_half = [own_bank("sums_p"), own_bank("sums_x")]
-                second_product(e, "p", [by_half[h][:, 0, :] for h in range(HALVES)])
-                second_product(e, "x", [by_half[h][:, 1, :] for h in range(HALVES)])
+                quantize_w1(e)
+                first, middle, final = own_bank("sums_p"), own_bank("sums_x"), own_bank("sums_p")
+                last_sums = {"p": [first[:, 0, :], final[:, 0, :]], "x": [middle[:, 0, :], final[:, 1, :]]}
+                second_product(e, "p", last_sums["p"])
+                second_product(e, "x", last_sums["x"])
                 scatter(prev, "x", 1)
                 for h in range(HALVES):
-                    for g, kind in enumerate("px"):
+                    for kind in "px":
                         staged[e, kind, h] = own_tile("staged", [C], F32)
-                        stage(by_half[h][:, g, :], staged[e, kind, h])
+                        stage(last_sums[kind][h], staged[e, kind, h])
             else:
                 open_pass(nxt, 0)
                 open_pass(nxt, 1)
                 round_w2(nxt, 0, 0, HALF_H)
                 if e == 0:
                     bank[e] = own_bank("turned")
-                seam = grp2[nxt][:, H - SEAM : H + SEAM, :].rearrange("p i t -> p (i t)").bitcast(F32)
-                dh[e] = seam.rearrange("j (u p) -> j u p", u=2)
+                dh[e] = seam_at(nxt, H)
                 gate_sums(e, 0, H)
                 turn(e)
                 round_w2(nxt, 0, HALF_H, H - SEAM)
@@ -337,11 +344,11 @@ def tile_moe_dub_none_kernel(
                 for h in range(HALVES):
                     staged[e, "p", h], staged[e, "x", h] = homes[:, h, :], homes[:, 2 + h, :]
                 if held:
-                    dh[nxt] = own_tile("dh", [2, P], F32)
+                    dh[nxt] = seam_at(nxt, PASSES * H)
                     gate_sums(nxt, 0, HALF_H)
 
         def add_and_store(adder, queue, h, c0, c1):
-            total = work.tile([P, c1 - c0], F32, name="total", bufs=5)
+            total = work.tile([P, c1 - c0], F32, name="total", bufs=7)
             adder.tensor_tensor(total[:], dx_win[h][:, c0:c1], dp_win[h][:, c0:c1], ADD)
             queue.dma_start(out=out[h * P : (h + 1) * P, c0:c1], in_=total[:])
 
@@ -350,6 +357,7 @@ def tile_moe_dub_none_kernel(
             scatter(E - 1, "x", h)
         add_and_store(nc.gpsimd, nc.scalar, 0, 0, GPSIMD_ADD)
         add_and_store(nc.gpsimd, nc.scalar, 0, GPSIMD_ADD, 2 * GPSIMD_ADD)
-        add_and_store(nc.vector, nc.sync, 0, 2 * GPSIMD_ADD, T)
-        add_and_store(nc.vector, nc.sync, 1, 0, T - LAST_ADD)
-        add_and_store(nc.vector, nc.sync, 1, T - LAST_ADD, T)
+        add_and_store(nc.vector, nc.sync, 0, 2 * GPSIMD_ADD, 3 * GPSIMD_ADD)
+        add_and_store(nc.vector, nc.sync, 0, 3 * GPSIMD_ADD, T)
+        for c0, c1 in zip(ADD_CUTS, ADD_CUTS[1:]):
+            add_and_store(nc.vector, nc.sync, 1, c0, c1)

@@ -29,8 +29,11 @@ HALF_H = H // 2
 QUARTER_H = H // 4
 GATHER_CUTS = (0, 2 * C, E * C)
 FIRST_LATE_W1 = E - 1
-SEAM = 64
-VECTOR_CUT = 384
+SEAM = 16
+W1_TAIL = 64
+PASS_STEP = H + C - SEAM
+GATE_CUT = 256
+VECTOR_CUT = 352
 GPSIMD_ADD = 256
 ADD_CUTS = (0, 384, 768, 1024)
 RAW_W2_BUFS = 11
@@ -133,9 +136,9 @@ def tile_moe_dub_none_kernel(
 
         def open_pass(e, s):
             if s == 0:
-                both = work.tile([P, PASSES * H + SEAM, PACK], BF16, name="grp2", align_bytes=64, bufs=GROUPED_BUFS)
+                both = work.tile([P, PASSES * PASS_STEP, PACK], BF16, name="grp2", align_bytes=64, bufs=GROUPED_BUFS)
                 grp2[e] = both[:]
-            grp2[e, s] = grp2[e][:, s * H : (s + 1) * H, :]
+            grp2[e, s] = grp2[e][:, s * PASS_STEP : s * PASS_STEP + H, :]
             codes = work.tile([P, H], U32, name="w2_codes", align_bytes=64)
             scales = work.tile([P, H], U8, name="w2_scales", align_bytes=64)
             w2q[e, s] = codes, scales
@@ -183,8 +186,9 @@ def tile_moe_dub_none_kernel(
                 stop=(s == PASSES - 1),
             )
 
-        def seam_at(e, column):
-            seam = grp2[e][:, column - SEAM : column + SEAM, :].rearrange("p i t -> p (i t)").bitcast(F32)
+        def seam_at(e, s, overlap):
+            first = s * PASS_STEP + H - overlap
+            seam = grp2[e][:, first : first + C, :].rearrange("p i t -> p (i t)").bitcast(F32)
             return seam.rearrange("j (u p) -> j u p", u=2)
 
         def gate_sums(e, c0, c1):
@@ -270,17 +274,13 @@ def tile_moe_dub_none_kernel(
         for e in range(E):
             nxt, prev = e + 1, e - 1
             last = nxt == E
-            if last:
-                quantize_w2(e, 1, HALF_H, VECTOR_CUT)
-                first_product(e, 1, HALF_H, H)
-            else:
-                quantize_w2(e, 1, HALF_H, H)
-                first_product(e, 1, 0, H)
+            quantize_w2(e, 1, HALF_H, H)
+            first_product(e, 1, HALF_H if last else 0, H)
             grp1[e] = grp2[e, 1][:, HALF_H:H, :]
             if e == 0:
                 interleave(nc.vector.tensor_copy, grp1[e], raw1[e][:])
             else:
-                wide = K - SEAM if last else K
+                wide = K - W1_TAIL if last else K
                 round_on_gpsimd(grp1[e][:, 0:wide, :], raw1[e][:, :, 0:wide])
             if e > 0:
                 scatters(prev, "p")
@@ -288,10 +288,12 @@ def tile_moe_dub_none_kernel(
                 if not last:
                     scatter(prev, "x", 1)
             if last:
+                dh[e] = seam_at(e, 1, W1_TAIL)
+                gate_sums(e, 0, HALF_H)
                 gate_sums(e, HALF_H, H)
                 turn(e)
                 copy_turned(e, own_tile("dh_t", [H], BF16))
-                interleave(nc.scalar.copy, grp1[e][:, K - SEAM : K, :], raw1[e][:, :, K - SEAM : K])
+                interleave(nc.scalar.copy, grp1[e][:, K - W1_TAIL : K, :], raw1[e][:, :, K - W1_TAIL : K])
                 staged[prev, "x", 1] = own_tile("staged", [C], F32)
                 stage(bank[e][:, 2, :], staged[prev, "x", 1])
                 quantize_dh(e)
@@ -308,13 +310,13 @@ def tile_moe_dub_none_kernel(
             else:
                 open_pass(nxt, 0)
                 open_pass(nxt, 1)
-                round_w2(nxt, 0, 0, HALF_H)
+                round_w2(nxt, 0, 0, GATE_CUT)
                 if e == 0:
                     bank[e] = own_bank("turned")
-                dh[e] = seam_at(nxt, H)
+                dh[e] = seam_at(nxt, 0, SEAM)
                 gate_sums(e, 0, H)
                 turn(e)
-                round_w2(nxt, 0, HALF_H, H - SEAM)
+                round_w2(nxt, 0, GATE_CUT, H - SEAM)
                 copy_turned(e, own_tile("dh_t", [H], BF16))
                 round_w2(nxt, 0, H - SEAM, H)
                 quantize_dh(e)
@@ -336,16 +338,12 @@ def tile_moe_dub_none_kernel(
                 quantize_w2(nxt, 1, 0, HALF_H)
                 if held:
                     first_product(nxt, 1, 0, HALF_H)
-                    quantize_w2(nxt, 1, VECTOR_CUT, H)
                 homes = raw2[nxt, 1][:, :, 0:C]
                 stage(sums_p[:, 0:2, :], homes[:, 0:2, :])
                 wide = 1 if held else 2
                 stage(sums_x[:, 0:wide, :], homes[:, 2 : 2 + wide, :])
                 for h in range(HALVES):
                     staged[e, "p", h], staged[e, "x", h] = homes[:, h, :], homes[:, 2 + h, :]
-                if held:
-                    dh[nxt] = seam_at(nxt, PASSES * H)
-                    gate_sums(nxt, 0, HALF_H)
 
         def add_and_store(adder, queue, h, c0, c1):
             total = work.tile([P, c1 - c0], F32, name="total", bufs=7)

@@ -30,6 +30,7 @@ QUARTER_H = H // 4
 GATHER_CUTS = (0, 2 * C, E * C)
 FIRST_LATE_W1 = E - 1
 SEAM = 16
+WP_CUTS = [0, 2, 4, 7]
 W1_TAIL = 64
 PASS_STEP = H + C - SEAM
 GATE_CUT = 256
@@ -92,17 +93,22 @@ def tile_moe_dub_none_kernel(
         def load_w2(e, s):
             raw2[e, s] = raw2_pool.tile([P, PACK, H], F32, name="raw2", align_bytes=64)
             rows = w2t[e, s * PASS : (s + 1) * PASS, :]
-            nc.sync.dma_start(out=raw2[e, s][:], in_=rows.rearrange("(p j) i -> p j i", j=PACK))
+            nc.sync.dma_start(
+                out=raw2[e, s][:].rearrange("p j i -> p (j i)"), in_=rows.rearrange("(p j) i -> p (j i)", j=PACK)
+            )
 
         def load_w1(e):
             raw1[e] = raw1_pool.tile([P, PACK, K], F32, name="raw1", align_bytes=64)
-            nc.sync.dma_start(out=raw1[e][:], in_=w1t[e].rearrange("(p j) k -> p j k", j=PACK))
+            nc.sync.dma_start(
+                out=raw1[e][:].rearrange("p j k -> p (j k)"), in_=w1t[e].rearrange("(p j) k -> p (j k)", j=PACK)
+            )
 
         def load_dy(s):
             nc.sync.dma_start(out=dy_win[s][:], in_=dy_words[s].rearrange("p t d -> p (t d)").bitcast(I32))
 
-        def load_wp(e):
-            nc.sync.dma_start(out=wp_words[:, e, :].bitcast(I32), in_=wpt_words[e, 0].bitcast(I32))
+        def load_wp(e0, e1):
+            words = wpt_words[e0:e1, 0].rearrange("e p b -> p e b")
+            nc.sync.dma_start(out=wp_words[:, e0:e1, :].bitcast(I32), in_=words.bitcast(I32))
 
         nc.sync.dma_start(token_list[:], offs)
         load_dy(0)
@@ -120,10 +126,11 @@ def tile_moe_dub_none_kernel(
             if e == 1:
                 nc.sync.dma_start(partner_list[:], offs2)
             load_w1(e - 1)
-            load_wp(e - 1)
+            if e - 1 in WP_CUTS:
+                load_wp(e - 1, WP_CUTS[WP_CUTS.index(e - 1) + 1])
             load_w2(e, 1)
         load_w1(E - 1)
-        load_wp(E - 1)
+        load_wp(E - 1, E)
 
         def picks(c):
             return token_list[:, GATHER_CUTS[c] // LIST_STEP : GATHER_CUTS[c + 1] // LIST_STEP]

@@ -24,22 +24,21 @@ PASS = P * PACK
 PASSES = N // PASS
 HALVES = K // P
 QUADRANTS = 4
+SCALE_ROWS = 4
 LIST_STEP = 16
 HALF_H = H // 2
-QUARTER_H = H // 4
 GATHER_CUTS = (0, 2 * C, E * C)
-FIRST_LATE_W1 = E - 1
-SEAM = 16
-WP_CUTS = [0, 2, 4, 7]
-W1_TAIL = 64
-PASS_STEP = H + C - SEAM
-GATE_CUT = 256
+WP_GROUPS = {0: 2, 2: 4, 4: E - 1}
 VECTOR_CUT = 352
+HELD_COLUMNS = 16
+HELD_W1_COLUMNS = 64
+PASS_STEP = H + C - HELD_COLUMNS
 GPSIMD_ADD = 256
-ADD_CUTS = (0, 384, 768, 1024)
+ADD_CUTS = (0, 384, 768, T)
+TOTAL_BUFS = 7
 RAW_W2_BUFS = 11
+ROUNDED_BUFS = 3
 WORK_BUFS = 4
-GROUPED_BUFS = 3
 
 
 def interleave(copy, grouped, raw):
@@ -82,13 +81,13 @@ def tile_moe_dub_none_kernel(
         make_identity(nc, ident[:])
         nc.gpsimd.memset(gate_rows[:], 0.0)
         nc.gpsimd.memset(wp_scales[:].rearrange("p e k -> p (e k)").bitcast(I32), 0)
-        for q in range(QUADRANTS):
+        for r in range(SCALE_ROWS):
             nc.gpsimd.dma_start(
-                out=wp_scales[32 * q : 32 * q + 4, :, :].bitcast(I32),
-                in_=wpt_scales[:, 0, 4 * q : 4 * q + 4, :].rearrange("e r k -> r e k").bitcast(I32),
+                out=wp_scales[r:P:32, :, :].bitcast(I32),
+                in_=wpt_scales[:, 0, r : QUADRANTS * SCALE_ROWS : SCALE_ROWS, :].rearrange("e q k -> q e k").bitcast(I32),
             )
 
-        raw2, raw1, grp2, grp1, w2q, w1q, acc, dh, bank, dh_t, dq, sums, staged = [{} for n in range(13)]
+        raw2, raw1, both_passes, grp2, grp1, w2q, w1q, acc, dh, bank, dh_t, dq, staged = [{} for n in range(13)]
 
         def load_w2(e, s):
             raw2[e, s] = raw2_pool.tile([P, PACK, H], F32, name="raw2", align_bytes=64)
@@ -114,8 +113,8 @@ def tile_moe_dub_none_kernel(
         load_dy(0)
         for q in range(QUADRANTS):
             nc.sync.dma_start(
-                out=dys_win[32 * q : 32 * q + 4 * PASSES, :].bitcast(I32),
-                in_=dy_scales[:, 4 * q : 4 * q + 4, :].bitcast(I32),
+                out=dys_win[32 * q : 32 * q + SCALE_ROWS * PASSES, :].bitcast(I32),
+                in_=dy_scales[:, SCALE_ROWS * q : SCALE_ROWS * (q + 1), :].bitcast(I32),
             )
         load_w2(0, 0)
         load_dy(1)
@@ -126,8 +125,8 @@ def tile_moe_dub_none_kernel(
             if e == 1:
                 nc.sync.dma_start(partner_list[:], offs2)
             load_w1(e - 1)
-            if e - 1 in WP_CUTS:
-                load_wp(e - 1, WP_CUTS[WP_CUTS.index(e - 1) + 1])
+            if e - 1 in WP_GROUPS:
+                load_wp(e - 1, WP_GROUPS[e - 1])
             load_w2(e, 1)
         load_w1(E - 1)
         load_wp(E - 1, E)
@@ -143,9 +142,10 @@ def tile_moe_dub_none_kernel(
 
         def open_pass(e, s):
             if s == 0:
-                both = work.tile([P, PASSES * PASS_STEP, PACK], BF16, name="grp2", align_bytes=64, bufs=GROUPED_BUFS)
-                grp2[e] = both[:]
-            grp2[e, s] = grp2[e][:, s * PASS_STEP : s * PASS_STEP + H, :]
+                both_passes[e] = work.tile(
+                    [P, PASSES * PASS_STEP, PACK], BF16, name="grp2", align_bytes=64, bufs=ROUNDED_BUFS
+                )
+            grp2[e, s] = both_passes[e][:, s * PASS_STEP : s * PASS_STEP + H, :]
             codes = work.tile([P, H], U32, name="w2_codes", align_bytes=64)
             scales = work.tile([P, H], U8, name="w2_scales", align_bytes=64)
             w2q[e, s] = codes, scales
@@ -186,17 +186,17 @@ def tile_moe_dub_none_kernel(
             nc.tensor.matmul_mx(
                 out=acc[e, c0][:],
                 lhsT=g_words[s][c][:, slots].bitcast(FP8X4),
-                lhsT_scale=g_scales[c][4 * s : P, slots],
+                lhsT_scale=g_scales[c][SCALE_ROWS * s : P, slots],
                 rhs=codes[:, c0:c1].bitcast(FP8X4),
                 rhs_scale=scales[:, c0:c1],
                 start=(s == 0),
                 stop=(s == PASSES - 1),
             )
 
-        def seam_at(e, s, overlap):
-            first = s * PASS_STEP + H - overlap
-            seam = grp2[e][:, first : first + C, :].rearrange("p i t -> p (i t)").bitcast(F32)
-            return seam.rearrange("j (u p) -> j u p", u=2)
+        def place_dh(e, s, held):
+            first = s * PASS_STEP + H - held
+            words = both_passes[e][:, first : first + C, :].rearrange("p i t -> p (i t)").bitcast(F32)
+            return words.rearrange("j (u p) -> j u p", u=2)
 
         def gate_sums(e, c0, c1):
             nc.scalar.activation(
@@ -210,8 +210,8 @@ def tile_moe_dub_none_kernel(
             for u in (1, 0):
                 nc.tensor.transpose(bank[e][:, u, :], dh[e][:, u, :], ident[:])
 
-        def copy_turned(e, home):
-            dh_t[e] = home
+        def copy_turned(e):
+            dh_t[e] = own_tile("dh_t", [H], BF16)
             nc.scalar.copy(
                 out=dh_t[e].bitcast(F32).rearrange("p (j u) -> p j u", u=2),
                 in_=bank[e][:, 0:2, :].rearrange("p u j -> p j u"),
@@ -260,6 +260,11 @@ def tile_moe_dub_none_kernel(
             fresh = work.tile([P] + shape, dtype, name=name, align_bytes=64)
             return fresh[:]
 
+        def add_and_store(adder, queue, h, c0, c1):
+            total = work.tile([P, c1 - c0], F32, name="total", bufs=TOTAL_BUFS)
+            adder.tensor_tensor(total[:], dx_win[h][:, c0:c1], dp_win[h][:, c0:c1], ADD)
+            queue.dma_start(out=out[h * P : (h + 1) * P, c0:c1], in_=total[:])
+
         gather_words(0, 0)
         gather_scales(0)
         gather_words(0, 1)
@@ -278,88 +283,86 @@ def tile_moe_dub_none_kernel(
         nc.scalar.activation(out=gate_cols[:], in_=gate_t[:, 0, 0:E], func=COPY)
         quantize_w2(0, 1, 0, HALF_H)
 
-        for e in range(E):
+        last = E - 1
+        for e in range(last):
             nxt, prev = e + 1, e - 1
-            last = nxt == E
             quantize_w2(e, 1, HALF_H, H)
-            first_product(e, 1, HALF_H if last else 0, H)
+            first_product(e, 1, 0, H)
             grp1[e] = grp2[e, 1][:, HALF_H:H, :]
             if e == 0:
                 interleave(nc.vector.tensor_copy, grp1[e], raw1[e][:])
             else:
-                wide = K - W1_TAIL if last else K
-                round_on_gpsimd(grp1[e][:, 0:wide, :], raw1[e][:, :, 0:wide])
-            if e > 0:
+                round_on_gpsimd(grp1[e], raw1[e][:])
                 scatters(prev, "p")
-                scatter(prev, "x", 0)
-                if not last:
-                    scatter(prev, "x", 1)
-            if last:
-                dh[e] = seam_at(e, 1, W1_TAIL)
-                gate_sums(e, 0, HALF_H)
-                gate_sums(e, HALF_H, H)
-                turn(e)
-                copy_turned(e, own_tile("dh_t", [H], BF16))
-                interleave(nc.scalar.copy, grp1[e][:, K - W1_TAIL : K, :], raw1[e][:, :, K - W1_TAIL : K])
-                staged[prev, "x", 1] = own_tile("staged", [C], F32)
-                stage(bank[e][:, 2, :], staged[prev, "x", 1])
-                quantize_dh(e)
-                quantize_w1(e)
-                first, middle, final = own_bank("sums_p"), own_bank("sums_x"), own_bank("sums_p")
-                last_sums = {"p": [first[:, 0, :], final[:, 0, :]], "x": [middle[:, 0, :], final[:, 1, :]]}
-                second_product(e, "p", last_sums["p"])
-                second_product(e, "x", last_sums["x"])
-                scatter(prev, "x", 1)
-                for h in range(HALVES):
-                    for kind in "px":
-                        staged[e, kind, h] = own_tile("staged", [C], F32)
-                        stage(last_sums[kind][h], staged[e, kind, h])
+                scatters(prev, "x")
+            open_pass(nxt, 0)
+            open_pass(nxt, 1)
+            round_w2(nxt, 0, 0, HALF_H)
+            if e == 0:
+                bank[e] = own_bank("turned")
+            dh[e] = place_dh(nxt, 0, HELD_COLUMNS)
+            gate_sums(e, 0, H)
+            turn(e)
+            round_w2(nxt, 0, HALF_H, H - HELD_COLUMNS)
+            copy_turned(e)
+            round_w2(nxt, 0, H - HELD_COLUMNS, H)
+            quantize_dh(e)
+            quantize_w1(e)
+            bank[nxt] = own_bank("turned")
+            sums_p, sums_x = own_bank("sums_p"), own_bank("sums_x")
+            second_product(e, "p", [sums_p[:, h, :] for h in range(HALVES)])
+            before_last = nxt == last
+            second_product(e, "x", [sums_x[:, 0, :], bank[nxt][:, 2, :] if before_last else sums_x[:, 1, :]])
+            quantize_w2(nxt, 0, 0, H)
+            if before_last:
+                first_product(nxt, 0, 0, HALF_H)
+                first_product(nxt, 0, HALF_H, H)
             else:
-                open_pass(nxt, 0)
-                open_pass(nxt, 1)
-                round_w2(nxt, 0, 0, GATE_CUT)
-                if e == 0:
-                    bank[e] = own_bank("turned")
-                dh[e] = seam_at(nxt, 0, SEAM)
-                gate_sums(e, 0, H)
-                turn(e)
-                round_w2(nxt, 0, GATE_CUT, H - SEAM)
-                copy_turned(e, own_tile("dh_t", [H], BF16))
-                round_w2(nxt, 0, H - SEAM, H)
-                quantize_dh(e)
-                quantize_w1(e)
-                bank[nxt] = own_bank("turned")
-                sums_p, sums_x = own_bank("sums_p"), own_bank("sums_x")
-                second_product(e, "p", [sums_p[:, h, :] for h in range(HALVES)])
-                held = nxt == E - 1
-                second_product(e, "x", [sums_x[:, 0, :], bank[nxt][:, 2, :] if held else sums_x[:, 1, :]])
-                quantize_w2(nxt, 0, 0, H)
-                if held:
-                    first_product(nxt, 0, 0, HALF_H)
-                    first_product(nxt, 0, HALF_H, H)
-                else:
-                    first_product(nxt, 0, 0, H)
-                round_w2(nxt, 1, VECTOR_CUT, H, nc.vector.tensor_copy)
-                round_w2(nxt, 1, 0, HALF_H)
-                round_w2(nxt, 1, HALF_H, VECTOR_CUT)
-                quantize_w2(nxt, 1, 0, HALF_H)
-                if held:
-                    first_product(nxt, 1, 0, HALF_H)
-                homes = raw2[nxt, 1][:, :, 0:C]
-                stage(sums_p[:, 0:2, :], homes[:, 0:2, :])
-                wide = 1 if held else 2
-                stage(sums_x[:, 0:wide, :], homes[:, 2 : 2 + wide, :])
-                for h in range(HALVES):
-                    staged[e, "p", h], staged[e, "x", h] = homes[:, h, :], homes[:, 2 + h, :]
+                first_product(nxt, 0, 0, H)
+            round_w2(nxt, 1, VECTOR_CUT, H, nc.vector.tensor_copy)
+            round_w2(nxt, 1, 0, HALF_H)
+            round_w2(nxt, 1, HALF_H, VECTOR_CUT)
+            quantize_w2(nxt, 1, 0, HALF_H)
+            if before_last:
+                first_product(nxt, 1, 0, HALF_H)
+            homes = raw2[nxt, 1][:, :, 0:C]
+            stage(sums_p[:, 0:HALVES, :], homes[:, 0:HALVES, :])
+            ready = 1 if before_last else HALVES
+            stage(sums_x[:, 0:ready, :], homes[:, HALVES : HALVES + ready, :])
+            for h in range(HALVES):
+                staged[e, "p", h], staged[e, "x", h] = homes[:, h, :], homes[:, HALVES + h, :]
 
-        def add_and_store(adder, queue, h, c0, c1):
-            total = work.tile([P, c1 - c0], F32, name="total", bufs=7)
-            adder.tensor_tensor(total[:], dx_win[h][:, c0:c1], dp_win[h][:, c0:c1], ADD)
-            queue.dma_start(out=out[h * P : (h + 1) * P, c0:c1], in_=total[:])
-
+        prev = last - 1
+        w1_cut = K - HELD_W1_COLUMNS
+        quantize_w2(last, 1, HALF_H, H)
+        first_product(last, 1, HALF_H, H)
+        grp1[last] = grp2[last, 1][:, HALF_H:H, :]
+        round_on_gpsimd(grp1[last][:, 0:w1_cut, :], raw1[last][:, :, 0:w1_cut])
+        scatters(prev, "p")
+        scatter(prev, "x", 0)
+        dh[last] = place_dh(last, 1, HELD_W1_COLUMNS)
+        gate_sums(last, 0, HALF_H)
+        gate_sums(last, HALF_H, H)
+        turn(last)
+        copy_turned(last)
+        interleave(nc.scalar.copy, grp1[last][:, w1_cut:K, :], raw1[last][:, :, w1_cut:K])
+        staged[prev, "x", 1] = own_tile("staged", [C], F32)
+        stage(bank[last][:, 2, :], staged[prev, "x", 1])
+        quantize_dh(last)
+        quantize_w1(last)
+        first, middle, final = own_bank("sums_p"), own_bank("sums_x"), own_bank("sums_p")
+        last_sums = {"p": [first[:, 0, :], final[:, 0, :]], "x": [middle[:, 0, :], final[:, 1, :]]}
+        second_product(last, "p", last_sums["p"])
+        second_product(last, "x", last_sums["x"])
+        scatter(prev, "x", 1)
         for h in range(HALVES):
-            scatter(E - 1, "p", h)
-            scatter(E - 1, "x", h)
+            for kind in "px":
+                staged[last, kind, h] = own_tile("staged", [C], F32)
+                stage(last_sums[kind][h], staged[last, kind, h])
+        for h in range(HALVES):
+            scatter(last, "p", h)
+            scatter(last, "x", h)
+
         add_and_store(nc.gpsimd, nc.scalar, 0, 0, GPSIMD_ADD)
         add_and_store(nc.gpsimd, nc.scalar, 0, GPSIMD_ADD, 2 * GPSIMD_ADD)
         add_and_store(nc.vector, nc.sync, 0, 2 * GPSIMD_ADD, 3 * GPSIMD_ADD)

@@ -32,7 +32,9 @@ WP_GROUPS = {0: 2, 2: 4, 4: E - 1}
 VECTOR_CUT = 352
 HELD_COLUMNS = 16
 HELD_W1_COLUMNS = 64
-PASS_STEP = H + C - HELD_COLUMNS
+LOW_END = HALF_H + C - HELD_COLUMNS
+GPSIMD_CUT = 320
+FIRST_CUT = 128
 GPSIMD_ADD = 256
 ADD_CUTS = (0, 384, 768, T)
 TOTAL_BUFS = 7
@@ -87,7 +89,7 @@ def tile_moe_dub_none_kernel(
                 in_=wpt_scales[:, 0, r : QUADRANTS * SCALE_ROWS : SCALE_ROWS, :].rearrange("e q k -> q e k").bitcast(I32),
             )
 
-        raw2, raw1, both_passes, grp2, grp1, w2q, w1q, acc, dh, bank, dh_t, dq, staged = [{} for n in range(13)]
+        raw2, raw1, rounded, grp2, grp1, w2q, w1q, acc, dh, bank, dh_t, dq, staged = [{} for n in range(13)]
 
         def load_w2(e, s):
             raw2[e, s] = raw2_pool.tile([P, PACK, H], F32, name="raw2", align_bytes=64)
@@ -140,29 +142,38 @@ def tile_moe_dub_none_kernel(
         def gather_scales(c):
             nc.vector.tensor_copy(g_scales[c][:], dys_win[:].indirect(picks(c)))
 
-        def open_pass(e, s):
-            if s == 0:
-                both_passes[e] = work.tile(
-                    [P, PASSES * PASS_STEP, PACK], BF16, name="grp2", align_bytes=64, bufs=ROUNDED_BUFS
-                )
-            grp2[e, s] = both_passes[e][:, s * PASS_STEP : s * PASS_STEP + H, :]
-            codes = work.tile([P, H], U32, name="w2_codes", align_bytes=64)
-            scales = work.tile([P, H], U8, name="w2_scales", align_bytes=64)
-            w2q[e, s] = codes, scales
+        def open_expert(e):
+            rounded[e] = work.tile(
+                [P, LOW_END + H + C - HELD_W1_COLUMNS, PACK], BF16, name="grp2", align_bytes=64, bufs=ROUNDED_BUFS
+            )
+            grp2[e, 0, 0] = rounded[e][:, 0:HALF_H, :]
+            for half in range(2):
+                grp2[e, 1, half] = rounded[e][:, LOW_END + half * HALF_H : LOW_END + (half + 1) * HALF_H, :]
+            for s in range(PASSES):
+                codes = work.tile([P, H], U32, name="w2_codes", align_bytes=64)
+                scales = work.tile([P, H], U8, name="w2_scales", align_bytes=64)
+                w2q[e, s] = codes, scales
 
         def round_on_gpsimd(grouped, raw):
             nc.gpsimd.tensor_scalar(grouped, raw.rearrange("p t c -> p c t"), 1.0, 0.0, MULT, ADD)
 
-        def round_w2(e, s, c0, c1, copy=nc.scalar.copy):
-            interleave(copy, grp2[e, s][:, c0:c1, :], raw2[e, s][:, :, c0:c1])
+        def columns(e, s, c0, c1):
+            half = c0 // HALF_H
+            return grp2[e, s, half][:, c0 - half * HALF_H : c1 - half * HALF_H, :]
 
-        def quantize_w2(e, s, c0, c1):
+        def round_w2(e, s, c0, c1, copy=nc.scalar.copy):
+            interleave(copy, columns(e, s, c0, c1), raw2[e, s][:, :, c0:c1])
+
+        def round_w2_on_gpsimd(e, s, c0, c1):
+            round_on_gpsimd(columns(e, s, c0, c1), raw2[e, s][:, :, c0:c1])
+
+        def quantize_w2(e, s, half):
             codes, scales = w2q[e, s]
-            cols = slice(c0, c1)
+            cols = slice(half * HALF_H, (half + 1) * HALF_H)
             nc.vector.quantize_mx(
                 out=codes[:, cols].bitcast(FP8X4),
                 scales=scales[:, cols],
-                in_=grp2[e, s][:, cols, :].rearrange("p i t -> p (i t)"),
+                in_=grp2[e, s, half].rearrange("p i t -> p (i t)"),
             )
 
         def quantize(values, width, tag):
@@ -193,9 +204,8 @@ def tile_moe_dub_none_kernel(
                 stop=(s == PASSES - 1),
             )
 
-        def place_dh(e, s, held):
-            first = s * PASS_STEP + H - held
-            words = both_passes[e][:, first : first + C, :].rearrange("p i t -> p (i t)").bitcast(F32)
+        def place_dh(e, first):
+            words = rounded[e][:, first : first + C, :].rearrange("p i t -> p (i t)").bitcast(F32)
             return words.rearrange("j (u p) -> j u p", u=2)
 
         def gate_sums(e, c0, c1):
@@ -256,8 +266,8 @@ def tile_moe_dub_none_kernel(
             for h in range(HALVES):
                 scatter(e, kind, h)
 
-        def own_tile(name, shape, dtype):
-            fresh = work.tile([P] + shape, dtype, name=name, align_bytes=64)
+        def own_tile(name, shape, dtype, bufs=WORK_BUFS):
+            fresh = work.tile([P] + shape, dtype, name=name, align_bytes=64, bufs=bufs)
             return fresh[:]
 
         def add_and_store(adder, queue, h, c0, c1):
@@ -270,42 +280,48 @@ def tile_moe_dub_none_kernel(
         gather_words(0, 1)
         gather_words(1, 0)
         gather_scales(1)
-        open_pass(0, 0)
-        round_w2(0, 0, 0, H)
-        quantize_w2(0, 0, 0, H)
+        open_expert(0)
+        grp2[0, 0, 1] = own_tile("first_high", [HALF_H, PACK], BF16, 1)
+        round_w2(0, 0, 0, HALF_H)
+        round_w2(0, 0, HALF_H, H)
+        quantize_w2(0, 0, 0)
+        quantize_w2(0, 0, 1)
         first_product(0, 0, 0, H)
         gather_words(1, 1)
-        open_pass(0, 1)
         round_w2(0, 1, 0, HALF_H)
         round_w2(0, 1, HALF_H, H)
         gate_t = own_bank("turned")
         nc.tensor.transpose(gate_t[:, 0, :], gate_rows[:], ident[:])
         nc.scalar.activation(out=gate_cols[:], in_=gate_t[:, 0, 0:E], func=COPY)
-        quantize_w2(0, 1, 0, HALF_H)
+        quantize_w2(0, 1, 0)
 
         last = E - 1
         for e in range(last):
             nxt, prev = e + 1, e - 1
-            quantize_w2(e, 1, HALF_H, H)
+            quantize_w2(e, 1, 1)
             first_product(e, 1, 0, H)
-            grp1[e] = grp2[e, 1][:, HALF_H:H, :]
+            open_expert(nxt)
+            grp2[nxt, 0, 1] = grp2[e, 1, 1]
+            grp1[e] = grp2[e, 1, 0]
             if e == 0:
+                round_w2(nxt, 0, GPSIMD_CUT, H, nc.vector.tensor_copy)
                 interleave(nc.vector.tensor_copy, grp1[e], raw1[e][:])
             else:
+                round_w2_on_gpsimd(nxt, 0, GPSIMD_CUT, H)
                 round_on_gpsimd(grp1[e], raw1[e][:])
                 scatters(prev, "p")
                 scatters(prev, "x")
-            open_pass(nxt, 0)
-            open_pass(nxt, 1)
-            round_w2(nxt, 0, 0, HALF_H)
+            round_w2(nxt, 0, 0, FIRST_CUT)
             if e == 0:
                 bank[e] = own_bank("turned")
-            dh[e] = place_dh(nxt, 0, HELD_COLUMNS)
+            dh[e] = place_dh(nxt, HALF_H - HELD_COLUMNS)
             gate_sums(e, 0, H)
             turn(e)
-            round_w2(nxt, 0, HALF_H, H - HELD_COLUMNS)
+            if GPSIMD_CUT > HALF_H:
+                round_w2(nxt, 0, HALF_H, GPSIMD_CUT)
+            round_w2(nxt, 0, FIRST_CUT, HALF_H - HELD_COLUMNS)
             copy_turned(e)
-            round_w2(nxt, 0, H - HELD_COLUMNS, H)
+            round_w2(nxt, 0, HALF_H - HELD_COLUMNS, HALF_H)
             quantize_dh(e)
             quantize_w1(e)
             bank[nxt] = own_bank("turned")
@@ -313,16 +329,18 @@ def tile_moe_dub_none_kernel(
             second_product(e, "p", [sums_p[:, h, :] for h in range(HALVES)])
             before_last = nxt == last
             second_product(e, "x", [sums_x[:, 0, :], bank[nxt][:, 2, :] if before_last else sums_x[:, 1, :]])
-            quantize_w2(nxt, 0, 0, H)
+            quantize_w2(nxt, 0, 1)
+            quantize_w2(nxt, 0, 0)
             if before_last:
                 first_product(nxt, 0, 0, HALF_H)
                 first_product(nxt, 0, HALF_H, H)
             else:
                 first_product(nxt, 0, 0, H)
-            round_w2(nxt, 1, VECTOR_CUT, H, nc.vector.tensor_copy)
+            if VECTOR_CUT < H:
+                round_w2(nxt, 1, VECTOR_CUT, H, nc.vector.tensor_copy)
             round_w2(nxt, 1, 0, HALF_H)
             round_w2(nxt, 1, HALF_H, VECTOR_CUT)
-            quantize_w2(nxt, 1, 0, HALF_H)
+            quantize_w2(nxt, 1, 0)
             if before_last:
                 first_product(nxt, 1, 0, HALF_H)
             homes = raw2[nxt, 1][:, :, 0:C]
@@ -334,13 +352,13 @@ def tile_moe_dub_none_kernel(
 
         prev = last - 1
         w1_cut = K - HELD_W1_COLUMNS
-        quantize_w2(last, 1, HALF_H, H)
+        quantize_w2(last, 1, 1)
         first_product(last, 1, HALF_H, H)
-        grp1[last] = grp2[last, 1][:, HALF_H:H, :]
+        grp1[last] = grp2[last, 1, 1]
         round_on_gpsimd(grp1[last][:, 0:w1_cut, :], raw1[last][:, :, 0:w1_cut])
         scatters(prev, "p")
         scatter(prev, "x", 0)
-        dh[last] = place_dh(last, 1, HELD_W1_COLUMNS)
+        dh[last] = place_dh(last, LOW_END + H - HELD_W1_COLUMNS)
         gate_sums(last, 0, HALF_H)
         gate_sums(last, HALF_H, H)
         turn(last)

@@ -107,19 +107,23 @@ def tile_moe_dub_none_kernel(
         def load_dy(s):
             nc.sync.dma_start(out=dy_win[s][:], in_=dy_words[s].rearrange("p t d -> p (t d)").bitcast(I32))
 
+        def load_dy_scales(s):
+            for r in range(SCALE_ROWS):
+                nc.sync.dma_start(
+                    out=dys_win[SCALE_ROWS * s + r : P : 32, :].bitcast(I32),
+                    in_=dy_scales[s, r : QUADRANTS * SCALE_ROWS : SCALE_ROWS, :].bitcast(I32),
+                )
+
         def load_wp(e0, e1):
             words = wpt_words[e0:e1, 0].rearrange("e p b -> p e b")
             nc.sync.dma_start(out=wp_words[:, e0:e1, :].bitcast(I32), in_=words.bitcast(I32))
 
         nc.sync.dma_start(token_list[:], offs)
         load_dy(0)
-        for q in range(QUADRANTS):
-            nc.sync.dma_start(
-                out=dys_win[32 * q : 32 * q + SCALE_ROWS * PASSES, :].bitcast(I32),
-                in_=dy_scales[:, SCALE_ROWS * q : SCALE_ROWS * (q + 1), :].bitcast(I32),
-            )
+        load_dy_scales(0)
         load_w2(0, 0)
         load_dy(1)
+        load_dy_scales(1)
         load_w2(0, 1)
         nc.sync.dma_start(out=gate_rows[0:E, :], in_=gate.rearrange("p (e u) -> (p e) u", u=C)[0:E, :])
         for e in range(1, E):

@@ -29,10 +29,10 @@ LIST_STEP = 16
 HALF_H = H // 2
 GATHER_CUTS = (0, 2 * C, E * C)
 WP_GROUPS = {0: 2, 2: 4, 4: E - 1}
-VECTOR_CUT = 352
+VECTOR_CUT = 336
 HELD_COLUMNS = 16
-HELD_W1_COLUMNS = 64
-LOW_END = HALF_H + C - HELD_COLUMNS
+HELD_W1_COLUMNS = 32
+PASS1_START = HALF_H + C - HELD_COLUMNS
 GPSIMD_CUT = 320
 FIRST_CUT = 128
 GPSIMD_ADD = 256
@@ -79,7 +79,7 @@ def tile_moe_dub_none_kernel(
         dx_win = [keep.tile([P, T], F32, name="dx_win%d" % h) for h in range(HALVES)]
         dp_win = [keep.tile([P, T], F32, name="dp_win%d" % h) for h in range(HALVES)]
 
-        nc.gpsimd.memset(dys_win[:].bitcast(I32), 0)
+        nc.vector.memset(dys_win[:].bitcast(I32), 0)
         make_identity(nc, ident[:])
         nc.gpsimd.memset(gate_rows[:], 0.0)
         nc.gpsimd.memset(wp_scales[:].rearrange("p e k -> p (e k)").bitcast(I32), 0)
@@ -148,11 +148,11 @@ def tile_moe_dub_none_kernel(
 
         def open_expert(e):
             rounded[e] = work.tile(
-                [P, LOW_END + H + C - HELD_W1_COLUMNS, PACK], BF16, name="grp2", align_bytes=64, bufs=ROUNDED_BUFS
+                [P, PASS1_START + H + C - HELD_W1_COLUMNS, PACK], BF16, name="grp2", align_bytes=64, bufs=ROUNDED_BUFS
             )
             grp2[e, 0, 0] = rounded[e][:, 0:HALF_H, :]
             for half in range(2):
-                grp2[e, 1, half] = rounded[e][:, LOW_END + half * HALF_H : LOW_END + (half + 1) * HALF_H, :]
+                grp2[e, 1, half] = rounded[e][:, PASS1_START + half * HALF_H : PASS1_START + (half + 1) * HALF_H, :]
             for s in range(PASSES):
                 codes = work.tile([P, H], U32, name="w2_codes", align_bytes=64)
                 scales = work.tile([P, H], U8, name="w2_scales", align_bytes=64)
@@ -321,8 +321,7 @@ def tile_moe_dub_none_kernel(
             dh[e] = place_dh(nxt, HALF_H - HELD_COLUMNS)
             gate_sums(e, 0, H)
             turn(e)
-            if GPSIMD_CUT > HALF_H:
-                round_w2(nxt, 0, HALF_H, GPSIMD_CUT)
+            round_w2(nxt, 0, HALF_H, GPSIMD_CUT)
             round_w2(nxt, 0, FIRST_CUT, HALF_H - HELD_COLUMNS)
             copy_turned(e)
             round_w2(nxt, 0, HALF_H - HELD_COLUMNS, HALF_H)
@@ -340,8 +339,7 @@ def tile_moe_dub_none_kernel(
                 first_product(nxt, 0, HALF_H, H)
             else:
                 first_product(nxt, 0, 0, H)
-            if VECTOR_CUT < H:
-                round_w2(nxt, 1, VECTOR_CUT, H, nc.vector.tensor_copy)
+            round_w2(nxt, 1, VECTOR_CUT, H, nc.vector.tensor_copy)
             round_w2(nxt, 1, 0, HALF_H)
             round_w2(nxt, 1, HALF_H, VECTOR_CUT)
             quantize_w2(nxt, 1, 0)
@@ -362,7 +360,7 @@ def tile_moe_dub_none_kernel(
         round_on_gpsimd(grp1[last][:, 0:w1_cut, :], raw1[last][:, :, 0:w1_cut])
         scatters(prev, "p")
         scatter(prev, "x", 0)
-        dh[last] = place_dh(last, LOW_END + H - HELD_W1_COLUMNS)
+        dh[last] = place_dh(last, PASS1_START + H - HELD_W1_COLUMNS)
         gate_sums(last, 0, HALF_H)
         gate_sums(last, HALF_H, H)
         turn(last)

@@ -27,18 +27,23 @@ QUADRANTS = 4
 SCALE_ROWS = 4
 LIST_STEP = 16
 HALF_H = H // 2
+PIECES = ((H - C, H), (0, HALF_H), (HALF_H, H - C))
+FINE_FROM = 6
+STEADY_CUT = 336
 GATHER_CUTS = (0, 2 * C, E * C)
-WP_GROUPS = {0: 2, 2: 4, 4: E - 1}
-VECTOR_CUT = 336
-HELD_COLUMNS = 16
+WP_GROUPS = {e: e + 1 for e in range(E - 1)}
+VECTOR_CUT = 256
+HELD_COLUMNS = 32
 HELD_W1_COLUMNS = 32
-PASS1_START = HALF_H + C - HELD_COLUMNS
-GPSIMD_CUT = 320
-FIRST_CUT = 128
+PASS1_START = 0
+GPSIMD_CUT = 352
+FIRST_CUT = 64
+DH_START = 2 * (HALF_H - HELD_COLUMNS)
+FRONT = DH_START + 2 * C - FIRST_CUT
 GPSIMD_ADD = 256
 ADD_CUTS = (0, 384, 768, T)
 TOTAL_BUFS = 7
-RAW_W2_BUFS = 11
+RAW_W2_BUFS = 5
 ROUNDED_BUFS = 3
 WORK_BUFS = 4
 
@@ -59,20 +64,33 @@ def tile_moe_dub_none_kernel(
         raw2_pool = ctx.enter_context(tc.tile_pool(name="raw2", bufs=RAW_W2_BUFS))
         raw1_pool = ctx.enter_context(tc.tile_pool(name="raw1", bufs=E))
         work = ctx.enter_context(tc.tile_pool(name="work", bufs=WORK_BUFS))
+        head = ctx.enter_context(tc.tile_pool(name="head", bufs=1))
         psum = ctx.enter_context(tc.psum_pool(name="psum", bufs=2))
 
         piece_widths = [b - a for a, b in zip(GATHER_CUTS, GATHER_CUTS[1:])]
         token_list = keep.tile([P, T // LIST_STEP], U16, name="token_list")
         partner_list = keep.tile([P, T // LIST_STEP], U16, name="partner_list")
-        dy_win = [keep.tile([P, T], I32, name="dy_win%d" % s, align_bytes=64) for s in range(PASSES)]
-        dys_win = keep.tile([P, T], U8, name="dys_win", align_bytes=64)
+        dy_win = [keep.tile([P, T], I32, name="dy_win%d" % s, align_bytes=256) for s in range(PASSES)]
+        dys_win = keep.tile([P, T], U8, name="dys_win", align_bytes=256)
+        first, rest = piece_widths
+        first_pass1 = head.tile([P, H + HALF_H, PACK], BF16, name="first_pass1", align_bytes=256, offset=0)
         g_words = [
-            [keep.tile([P, w], U32, name="g_words%d_%d" % (s, c), align_bytes=64) for c, w in enumerate(piece_widths)]
-            for s in range(PASSES)
+            [
+                keep.tile([P, first], U32, name="g_words0_0", align_bytes=256),
+                keep.tile([P, rest], U32, name="g_words0_1", align_bytes=256),
+            ],
+            [
+                keep.tile([P, first], U32, name="g_words1_0", align_bytes=256),
+                keep.tile([P, rest], U32, name="g_words1_1", align_bytes=256),
+            ],
         ]
-        g_scales = [keep.tile([P, w], U8, name="g_scales%d" % c, align_bytes=64) for c, w in enumerate(piece_widths)]
-        wp_words = keep.tile([P, E, 2 * K], U8, name="wp_words", align_bytes=64)
-        wp_scales = keep.tile([P, E, K], U8, name="wp_scales", align_bytes=64)
+        g_scales = [
+            keep.tile([P, first], U8, name="g_scales0", align_bytes=256),
+            head.tile([P, rest], U8, name="g_scales1", align_bytes=256, offset=4 * rest),
+        ]
+        second_high = head.tile([P, HALF_H, PACK], BF16, name="second_high", align_bytes=256, offset=2 * PACK * H)
+        wp_words = keep.tile([P, E, 2 * K], U8, name="wp_words", align_bytes=256)
+        wp_scales = keep.tile([P, E, K], U8, name="wp_scales", align_bytes=256)
         gate_rows = keep.tile([P, C], F32, name="gate_rows")
         gate_cols = keep.tile([P, E], F32, name="gate_cols")
         ident = keep.tile([P, P], F32, name="ident")
@@ -89,17 +107,17 @@ def tile_moe_dub_none_kernel(
                 in_=wpt_scales[:, 0, r : QUADRANTS * SCALE_ROWS : SCALE_ROWS, :].rearrange("e q k -> q e k").bitcast(I32),
             )
 
-        raw2, raw1, rounded, grp2, grp1, w2q, w1q, acc, dh, bank, dh_t, dq, staged = [{} for n in range(13)]
+        flat2, raw2, raw1, rounded, grp2, grp1, w2q, w1q, acc, dh, bank, dh_t, dq, staged = [{} for n in range(14)]
 
         def load_w2(e, s):
-            raw2[e, s] = raw2_pool.tile([P, PACK, H], F32, name="raw2", align_bytes=64)
+            front = FRONT if s == 0 else 0
+            flat2[e, s] = raw2_pool.tile([P, front + PACK * H], F32, name="raw2_pass%d" % s, align_bytes=256)
+            raw2[e, s] = flat2[e, s][:, front:].rearrange("p (j i) -> p j i", j=PACK)
             rows = w2t[e, s * PASS : (s + 1) * PASS, :]
-            nc.sync.dma_start(
-                out=raw2[e, s][:].rearrange("p j i -> p (j i)"), in_=rows.rearrange("(p j) i -> p (j i)", j=PACK)
-            )
+            nc.sync.dma_start(out=flat2[e, s][:, front:], in_=rows.rearrange("(p j) i -> p (j i)", j=PACK))
 
         def load_w1(e):
-            raw1[e] = raw1_pool.tile([P, PACK, K], F32, name="raw1", align_bytes=64)
+            raw1[e] = raw1_pool.tile([P, PACK, K], F32, name="raw1", align_bytes=256)
             nc.sync.dma_start(
                 out=raw1[e][:].rearrange("p j k -> p (j k)"), in_=w1t[e].rearrange("(p j) k -> p (j k)", j=PACK)
             )
@@ -120,9 +138,9 @@ def tile_moe_dub_none_kernel(
 
         nc.sync.dma_start(token_list[:], offs)
         load_dy(0)
+        load_dy(1)
         load_dy_scales(0)
         load_w2(0, 0)
-        load_dy(1)
         load_dy_scales(1)
         load_w2(0, 1)
         nc.sync.dma_start(out=gate_rows[0:E, :], in_=gate.rearrange("p (e u) -> (p e) u", u=C)[0:E, :])
@@ -148,14 +166,14 @@ def tile_moe_dub_none_kernel(
 
         def open_expert(e):
             rounded[e] = work.tile(
-                [P, PASS1_START + H + C - HELD_W1_COLUMNS, PACK], BF16, name="grp2", align_bytes=64, bufs=ROUNDED_BUFS
+                [P, PASS1_START + H + C - HELD_W1_COLUMNS, PACK], BF16, name="grp2", align_bytes=256, bufs=ROUNDED_BUFS
             )
-            grp2[e, 0, 0] = rounded[e][:, 0:HALF_H, :]
+            grp2[e, 0, 0] = flat2[e, 0][:, 0:H].bitcast(BF16).rearrange("p (i t) -> p i t", t=PACK)
             for half in range(2):
                 grp2[e, 1, half] = rounded[e][:, PASS1_START + half * HALF_H : PASS1_START + (half + 1) * HALF_H, :]
             for s in range(PASSES):
-                codes = work.tile([P, H], U32, name="w2_codes", align_bytes=64)
-                scales = work.tile([P, H], U8, name="w2_scales", align_bytes=64)
+                codes = work.tile([P, H], U32, name="w2_codes", align_bytes=256)
+                scales = work.tile([P, H], U8, name="w2_scales", align_bytes=256)
                 w2q[e, s] = codes, scales
 
         def round_on_gpsimd(grouped, raw):
@@ -180,9 +198,25 @@ def tile_moe_dub_none_kernel(
                 in_=grp2[e, s, half].rearrange("p i t -> p (i t)"),
             )
 
+        def pass1_columns(e, c0, c1):
+            if e == 0:
+                return first_pass1[:, c0:c1, :]
+            return rounded[e][:, PASS1_START + c0 : PASS1_START + c1, :]
+
+        def round_pass1(e, c0, c1, copy):
+            interleave(copy, pass1_columns(e, c0, c1), raw2[e, 1][:, :, c0:c1])
+
+        def quantize_pass1(e, c0, c1):
+            codes, scales = w2q[e, 1]
+            nc.vector.quantize_mx(
+                out=codes[:, c0:c1].bitcast(FP8X4),
+                scales=scales[:, c0:c1],
+                in_=pass1_columns(e, c0, c1).rearrange("p i t -> p (i t)"),
+            )
+
         def quantize(values, width, tag):
-            codes = work.tile([P, width], U32, name=tag + "_codes", align_bytes=64)
-            scales = work.tile([P, width], U8, name=tag + "_scales", align_bytes=64)
+            codes = work.tile([P, width], U32, name=tag + "_codes", align_bytes=256)
+            scales = work.tile([P, width], U8, name=tag + "_scales", align_bytes=256)
             nc.vector.quantize_mx(out=codes[:].bitcast(FP8X4), scales=scales[:], in_=values)
             return codes, scales
 
@@ -192,9 +226,10 @@ def tile_moe_dub_none_kernel(
         def quantize_w1(e):
             w1q[e] = quantize(grp1[e].rearrange("p k t -> p (k t)"), K, "w1")
 
+        def open_sums(e, c0, c1):
+            acc[e, c0] = psum.tile([P, c1 - c0], F32, name="acc")
+
         def first_product(e, s, c0, c1):
-            if s == 0:
-                acc[e, c0] = psum.tile([P, c1 - c0], F32, name="acc")
             c = 0 if e * C < GATHER_CUTS[1] else 1
             slots = slice(e * C - GATHER_CUTS[c], (e + 1) * C - GATHER_CUTS[c])
             codes, scales = w2q[e, s]
@@ -271,43 +306,63 @@ def tile_moe_dub_none_kernel(
                 scatter(e, kind, h)
 
         def own_tile(name, shape, dtype, bufs=WORK_BUFS):
-            fresh = work.tile([P] + shape, dtype, name=name, align_bytes=64, bufs=bufs)
+            fresh = work.tile([P] + shape, dtype, name=name, align_bytes=256, bufs=bufs)
             return fresh[:]
 
         def add_and_store(adder, queue, h, c0, c1):
-            total = work.tile([P, c1 - c0], F32, name="total", bufs=TOTAL_BUFS)
+            total = work.tile([P, c1 - c0], F32, name="total", bufs=TOTAL_BUFS, align_bytes=256)
             adder.tensor_tensor(total[:], dx_win[h][:, c0:c1], dp_win[h][:, c0:c1], ADD)
             queue.dma_start(out=out[h * P : (h + 1) * P, c0:c1], in_=total[:])
+
+        def round_and_begin(e):
+            if e < FINE_FROM:
+                round_pass1(e, STEADY_CUT, H, nc.vector.tensor_copy)
+                round_pass1(e, 0, HALF_H, nc.scalar.copy)
+                round_pass1(e, HALF_H, STEADY_CUT, nc.scalar.copy)
+                quantize_pass1(e, 0, HALF_H)
+                return
+            round_pass1(e, 0, C, nc.vector.tensor_copy)
+            round_pass1(e, C, H - VECTOR_CUT, nc.vector.tensor_copy)
+            round_pass1(e, H - C, H, nc.scalar.copy)
+            if H - VECTOR_CUT < HALF_H:
+                round_pass1(e, H - VECTOR_CUT, HALF_H, nc.scalar.copy)
+            round_pass1(e, HALF_H, H - C, nc.scalar.copy)
+            quantize_pass1(e, 0, C)
+            quantize_pass1(e, H - C, H)
+            if e == E - 1:
+                first_product(e, 1, H - C, H)
+            quantize_pass1(e, C, HALF_H)
+            if e == E - 1:
+                first_product(e, 1, 0, HALF_H)
 
         gather_words(0, 0)
         gather_scales(0)
         gather_words(0, 1)
         gather_words(1, 0)
-        gather_scales(1)
+        gather_words(1, 1)
         open_expert(0)
         grp2[0, 0, 1] = own_tile("first_high", [HALF_H, PACK], BF16, 1)
         round_w2(0, 0, 0, HALF_H)
         round_w2(0, 0, HALF_H, H)
         quantize_w2(0, 0, 0)
         quantize_w2(0, 0, 1)
+        open_sums(0, 0, H)
         first_product(0, 0, 0, H)
-        gather_words(1, 1)
-        round_w2(0, 1, 0, HALF_H)
-        round_w2(0, 1, HALF_H, H)
+        round_and_begin(0)
         gate_t = own_bank("turned")
         nc.tensor.transpose(gate_t[:, 0, :], gate_rows[:], ident[:])
         nc.scalar.activation(out=gate_cols[:], in_=gate_t[:, 0, 0:E], func=COPY)
-        quantize_w2(0, 1, 0)
 
         last = E - 1
         for e in range(last):
             nxt, prev = e + 1, e - 1
-            quantize_w2(e, 1, 1)
+            quantize_pass1(e, HALF_H, H if e < FINE_FROM else H - C)
             first_product(e, 1, 0, H)
             open_expert(nxt)
-            grp2[nxt, 0, 1] = grp2[e, 1, 1]
+            grp2[nxt, 0, 1] = grp2[e, 1, 1] if e else second_high[:]
             grp1[e] = grp2[e, 1, 0]
             if e == 0:
+                gather_scales(1)
                 round_w2(nxt, 0, GPSIMD_CUT, H, nc.vector.tensor_copy)
                 interleave(nc.vector.tensor_copy, grp1[e], raw1[e][:])
             else:
@@ -316,13 +371,14 @@ def tile_moe_dub_none_kernel(
                 scatters(prev, "p")
                 scatters(prev, "x")
             round_w2(nxt, 0, 0, FIRST_CUT)
+            round_w2(nxt, 0, FIRST_CUT, 2 * FIRST_CUT)
             if e == 0:
                 bank[e] = own_bank("turned")
-            dh[e] = place_dh(nxt, HALF_H - HELD_COLUMNS)
+            dh[e] = flat2[nxt, 0][:, DH_START : DH_START + 2 * C].rearrange("j (u p) -> j u p", u=2)
             gate_sums(e, 0, H)
             turn(e)
             round_w2(nxt, 0, HALF_H, GPSIMD_CUT)
-            round_w2(nxt, 0, FIRST_CUT, HALF_H - HELD_COLUMNS)
+            round_w2(nxt, 0, 2 * FIRST_CUT, HALF_H - HELD_COLUMNS)
             copy_turned(e)
             round_w2(nxt, 0, HALF_H - HELD_COLUMNS, HALF_H)
             quantize_dh(e)
@@ -335,18 +391,20 @@ def tile_moe_dub_none_kernel(
             quantize_w2(nxt, 0, 1)
             quantize_w2(nxt, 0, 0)
             if before_last:
-                first_product(nxt, 0, 0, HALF_H)
-                first_product(nxt, 0, HALF_H, H)
+                for c0, c1 in PIECES:
+                    acc[nxt, c0] = psum.tile([P, c1 - c0], F32, name="acc" if c0 < H - C else "sums_x")
+                for c0, c1 in PIECES:
+                    first_product(nxt, 0, c0, c1)
             else:
+                open_sums(nxt, 0, H)
                 first_product(nxt, 0, 0, H)
-            round_w2(nxt, 1, VECTOR_CUT, H, nc.vector.tensor_copy)
-            round_w2(nxt, 1, 0, HALF_H)
-            round_w2(nxt, 1, HALF_H, VECTOR_CUT)
-            quantize_w2(nxt, 1, 0)
-            if before_last:
-                first_product(nxt, 1, 0, HALF_H)
-            homes = raw2[nxt, 1][:, :, 0:C]
-            stage(sums_p[:, 0:HALVES, :], homes[:, 0:HALVES, :])
+            round_and_begin(nxt)
+            homes = raw2[nxt, 1][:, :, 0:C] if nxt < FINE_FROM else raw2[nxt, 1][:, :, H - C : H]
+            if nxt < FINE_FROM:
+                stage(sums_p[:, 0:HALVES, :], homes[:, 0:HALVES, :])
+            else:
+                for h in range(HALVES):
+                    stage(sums_p[:, h, :], homes[:, h, :])
             ready = 1 if before_last else HALVES
             stage(sums_x[:, 0:ready, :], homes[:, HALVES : HALVES + ready, :])
             for h in range(HALVES):
@@ -354,15 +412,15 @@ def tile_moe_dub_none_kernel(
 
         prev = last - 1
         w1_cut = K - HELD_W1_COLUMNS
-        quantize_w2(last, 1, 1)
-        first_product(last, 1, HALF_H, H)
+        quantize_pass1(last, *PIECES[2])
+        first_product(last, 1, *PIECES[2])
         grp1[last] = grp2[last, 1, 1]
         round_on_gpsimd(grp1[last][:, 0:w1_cut, :], raw1[last][:, :, 0:w1_cut])
         scatters(prev, "p")
         scatter(prev, "x", 0)
         dh[last] = place_dh(last, PASS1_START + H - HELD_W1_COLUMNS)
-        gate_sums(last, 0, HALF_H)
-        gate_sums(last, HALF_H, H)
+        for c0, c1 in PIECES:
+            gate_sums(last, c0, c1)
         turn(last)
         copy_turned(last)
         interleave(nc.scalar.copy, grp1[last][:, w1_cut:K, :], raw1[last][:, :, w1_cut:K])

@@ -25,27 +25,25 @@ PASSES = N // PASS
 HALVES = K // P
 QUADRANTS = 4
 SCALE_ROWS = 4
+DY_SCALE_ROW = 8
 LIST_STEP = 16
+ALIGN = 256
 HALF_H = H // 2
-PIECES = ((H - C, H), (0, HALF_H), (HALF_H, H - C))
-FINE_FROM = 6
-STEADY_CUT = 336
+QUARTER_H = H // 4
 GATHER_CUTS = (0, 2 * C, E * C)
-WP_GROUPS = {e: e + 1 for e in range(E - 1)}
-VECTOR_CUT = 256
-HELD_COLUMNS = 32
-HELD_W1_COLUMNS = 32
-PASS1_START = 0
+STEADY_CUT = 336
+FINE_FROM = 5
+LAST_PIECES = ((H - QUARTER_H, H), (0, HALF_H), (HALF_H, H - QUARTER_H))
 GPSIMD_CUT = 352
-FIRST_CUT = 64
+FIRST_PIECE = 64
+HELD_COLUMNS = 32
 DH_START = 2 * (HALF_H - HELD_COLUMNS)
-FRONT = DH_START + 2 * C - FIRST_CUT
-GPSIMD_ADD = 256
-ADD_CUTS = (0, 384, 768, T)
-TOTAL_BUFS = 7
+FRONT = DH_START + 2 * C - FIRST_PIECE
+HELD_W1_COLUMNS = 32
 RAW_W2_BUFS = 5
 ROUNDED_BUFS = 3
 WORK_BUFS = 4
+TOTAL_BUFS = 5
 
 
 def interleave(copy, grouped, raw):
@@ -59,6 +57,7 @@ def tile_moe_dub_none_kernel(
     tc, dy_words, dy_scales, w2t, w1t, wpt_words, wpt_scales, gate, offs, offs2, out
 ):
     nc = tc.nc
+    last = E - 1
     with ExitStack() as ctx:
         keep = ctx.enter_context(tc.tile_pool(name="keep", bufs=1))
         raw2_pool = ctx.enter_context(tc.tile_pool(name="raw2", bufs=RAW_W2_BUFS))
@@ -68,30 +67,22 @@ def tile_moe_dub_none_kernel(
         psum = ctx.enter_context(tc.psum_pool(name="psum", bufs=2))
 
         piece_widths = [b - a for a, b in zip(GATHER_CUTS, GATHER_CUTS[1:])]
-        token_list = keep.tile([P, T // LIST_STEP], U16, name="token_list")
-        partner_list = keep.tile([P, T // LIST_STEP], U16, name="partner_list")
-        dy_win = [keep.tile([P, T], I32, name="dy_win%d" % s, align_bytes=256) for s in range(PASSES)]
-        dys_win = keep.tile([P, T], U8, name="dys_win", align_bytes=256)
-        first, rest = piece_widths
-        first_pass1 = head.tile([P, H + HALF_H, PACK], BF16, name="first_pass1", align_bytes=256, offset=0)
+        token_list = keep.tile([P, T // LIST_STEP], U16, name="token_list", align_bytes=ALIGN)
+        partner_list = keep.tile([P, T // LIST_STEP], U16, name="partner_list", align_bytes=ALIGN)
+        dy_win = [keep.tile([P, T], I32, name="dy_win%d" % s, align_bytes=ALIGN) for s in range(PASSES)]
+        dys_win = keep.tile([P, T], U8, name="dys_win", align_bytes=ALIGN)
         g_words = [
-            [
-                keep.tile([P, first], U32, name="g_words0_0", align_bytes=256),
-                keep.tile([P, rest], U32, name="g_words0_1", align_bytes=256),
-            ],
-            [
-                keep.tile([P, first], U32, name="g_words1_0", align_bytes=256),
-                keep.tile([P, rest], U32, name="g_words1_1", align_bytes=256),
-            ],
+            [keep.tile([P, w], U32, name="g_words%d_%d" % (s, c), align_bytes=ALIGN) for c, w in enumerate(piece_widths)]
+            for s in range(PASSES)
         ]
+        first_pass1 = head.tile([P, H, PACK], BF16, name="first_pass1", align_bytes=ALIGN, offset=0)
         g_scales = [
-            keep.tile([P, first], U8, name="g_scales0", align_bytes=256),
-            head.tile([P, rest], U8, name="g_scales1", align_bytes=256, offset=4 * rest),
+            keep.tile([P, piece_widths[0]], U8, name="g_scales0", align_bytes=ALIGN),
+            head.tile([P, piece_widths[1]], U8, name="g_scales1", align_bytes=ALIGN, offset=0),
         ]
-        second_high = head.tile([P, HALF_H, PACK], BF16, name="second_high", align_bytes=256, offset=2 * PACK * H)
-        wp_words = keep.tile([P, E, 2 * K], U8, name="wp_words", align_bytes=256)
-        wp_scales = keep.tile([P, E, K], U8, name="wp_scales", align_bytes=256)
-        gate_rows = keep.tile([P, C], F32, name="gate_rows")
+        wp_words = keep.tile([P, E, 2 * K], U8, name="wp_words", align_bytes=ALIGN)
+        wp_scales = keep.tile([P, E, K], U8, name="wp_scales", align_bytes=ALIGN)
+        gate_rows = keep.tile([P, C], F32, name="gate_rows", align_bytes=ALIGN)
         gate_cols = keep.tile([P, E], F32, name="gate_cols")
         ident = keep.tile([P, P], F32, name="ident")
         dx_win = [keep.tile([P, T], F32, name="dx_win%d" % h) for h in range(HALVES)]
@@ -107,17 +98,18 @@ def tile_moe_dub_none_kernel(
                 in_=wpt_scales[:, 0, r : QUADRANTS * SCALE_ROWS : SCALE_ROWS, :].rearrange("e q k -> q e k").bitcast(I32),
             )
 
-        flat2, raw2, raw1, rounded, grp2, grp1, w2q, w1q, acc, dh, bank, dh_t, dq, staged = [{} for n in range(14)]
+        w2_tile, raw2, raw1, spent, pass0, pass1, grp1 = [{} for n in range(7)]
+        w2q, w1q, acc, dh, bank, dh_t, dq, staged = [{} for n in range(8)]
 
         def load_w2(e, s):
             front = FRONT if s == 0 else 0
-            flat2[e, s] = raw2_pool.tile([P, front + PACK * H], F32, name="raw2_pass%d" % s, align_bytes=256)
-            raw2[e, s] = flat2[e, s][:, front:].rearrange("p (j i) -> p j i", j=PACK)
+            w2_tile[e, s] = raw2_pool.tile([P, front + PACK * H], F32, name="raw2_pass%d" % s, align_bytes=ALIGN)
+            raw2[e, s] = w2_tile[e, s][:, front:].rearrange("p (j i) -> p j i", j=PACK)
             rows = w2t[e, s * PASS : (s + 1) * PASS, :]
-            nc.sync.dma_start(out=flat2[e, s][:, front:], in_=rows.rearrange("(p j) i -> p (j i)", j=PACK))
+            nc.sync.dma_start(out=w2_tile[e, s][:, front:], in_=rows.rearrange("(p j) i -> p (j i)", j=PACK))
 
         def load_w1(e):
-            raw1[e] = raw1_pool.tile([P, PACK, K], F32, name="raw1", align_bytes=256)
+            raw1[e] = raw1_pool.tile([P, PACK, K], F32, name="raw1", align_bytes=ALIGN)
             nc.sync.dma_start(
                 out=raw1[e][:].rearrange("p j k -> p (j k)"), in_=w1t[e].rearrange("(p j) k -> p (j k)", j=PACK)
             )
@@ -128,13 +120,12 @@ def tile_moe_dub_none_kernel(
         def load_dy_scales(s):
             for r in range(SCALE_ROWS):
                 nc.sync.dma_start(
-                    out=dys_win[SCALE_ROWS * s + r : P : 32, :].bitcast(I32),
+                    out=dys_win[DY_SCALE_ROW + SCALE_ROWS * s + r : P : 32, :].bitcast(I32),
                     in_=dy_scales[s, r : QUADRANTS * SCALE_ROWS : SCALE_ROWS, :].bitcast(I32),
                 )
 
-        def load_wp(e0, e1):
-            words = wpt_words[e0:e1, 0].rearrange("e p b -> p e b")
-            nc.sync.dma_start(out=wp_words[:, e0:e1, :].bitcast(I32), in_=words.bitcast(I32))
+        def load_wp(e):
+            nc.sync.dma_start(out=wp_words[:, e, :].bitcast(I32), in_=wpt_words[e, 0].bitcast(I32))
 
         nc.sync.dma_start(token_list[:], offs)
         load_dy(0)
@@ -149,11 +140,18 @@ def tile_moe_dub_none_kernel(
             if e == 1:
                 nc.sync.dma_start(partner_list[:], offs2)
             load_w1(e - 1)
-            if e - 1 in WP_GROUPS:
-                load_wp(e - 1, WP_GROUPS[e - 1])
+            load_wp(e - 1)
             load_w2(e, 1)
-        load_w1(E - 1)
-        load_wp(E - 1, E)
+        load_w1(last)
+        load_wp(last)
+
+        def own_tile(name, shape, dtype, bufs=WORK_BUFS):
+            fresh = work.tile([P] + shape, dtype, name=name, align_bytes=ALIGN, bufs=bufs)
+            return fresh[:]
+
+        def own_bank(name):
+            fresh = psum.tile([P, 4, C], F32, name=name)
+            return fresh[:]
 
         def picks(c):
             return token_list[:, GATHER_CUTS[c] // LIST_STEP : GATHER_CUTS[c + 1] // LIST_STEP]
@@ -164,60 +162,37 @@ def tile_moe_dub_none_kernel(
         def gather_scales(c):
             nc.vector.tensor_copy(g_scales[c][:], dys_win[:].indirect(picks(c)))
 
-        def open_expert(e):
-            rounded[e] = work.tile(
-                [P, PASS1_START + H + C - HELD_W1_COLUMNS, PACK], BF16, name="grp2", align_bytes=256, bufs=ROUNDED_BUFS
-            )
-            grp2[e, 0, 0] = flat2[e, 0][:, 0:H].bitcast(BF16).rearrange("p (i t) -> p i t", t=PACK)
-            for half in range(2):
-                grp2[e, 1, half] = rounded[e][:, PASS1_START + half * HALF_H : PASS1_START + (half + 1) * HALF_H, :]
+        def open_expert(e, high_home):
+            spent[e] = own_tile("rounded", [H + C - HELD_W1_COLUMNS, PACK], BF16, ROUNDED_BUFS)
+            low_home = w2_tile[e, 0][:, 0:H].bitcast(BF16).rearrange("p (i t) -> p i t", t=PACK)
+            pass0[e] = low_home, high_home
+            pass1[e] = spent[e][:, 0:H, :] if e else first_pass1[:]
             for s in range(PASSES):
-                codes = work.tile([P, H], U32, name="w2_codes", align_bytes=256)
-                scales = work.tile([P, H], U8, name="w2_scales", align_bytes=256)
-                w2q[e, s] = codes, scales
-
-        def round_on_gpsimd(grouped, raw):
-            nc.gpsimd.tensor_scalar(grouped, raw.rearrange("p t c -> p c t"), 1.0, 0.0, MULT, ADD)
+                w2q[e, s] = own_tile("w2_codes", [H], U32), own_tile("w2_scales", [H], U8)
 
         def columns(e, s, c0, c1):
+            if s == 1:
+                return pass1[e][:, c0:c1, :]
             half = c0 // HALF_H
-            return grp2[e, s, half][:, c0 - half * HALF_H : c1 - half * HALF_H, :]
+            return pass0[e][half][:, c0 - half * HALF_H : c1 - half * HALF_H, :]
 
         def round_w2(e, s, c0, c1, copy=nc.scalar.copy):
             interleave(copy, columns(e, s, c0, c1), raw2[e, s][:, :, c0:c1])
 
-        def round_w2_on_gpsimd(e, s, c0, c1):
-            round_on_gpsimd(columns(e, s, c0, c1), raw2[e, s][:, :, c0:c1])
+        def round_on_gpsimd(grouped, raw):
+            nc.gpsimd.tensor_scalar(grouped, raw.rearrange("p t c -> p c t"), 1.0, 0.0, MULT, ADD)
 
-        def quantize_w2(e, s, half):
+        def quantize_w2(e, s, c0, c1):
             codes, scales = w2q[e, s]
-            cols = slice(half * HALF_H, (half + 1) * HALF_H)
-            nc.vector.quantize_mx(
-                out=codes[:, cols].bitcast(FP8X4),
-                scales=scales[:, cols],
-                in_=grp2[e, s, half].rearrange("p i t -> p (i t)"),
-            )
-
-        def pass1_columns(e, c0, c1):
-            if e == 0:
-                return first_pass1[:, c0:c1, :]
-            return rounded[e][:, PASS1_START + c0 : PASS1_START + c1, :]
-
-        def round_pass1(e, c0, c1, copy):
-            interleave(copy, pass1_columns(e, c0, c1), raw2[e, 1][:, :, c0:c1])
-
-        def quantize_pass1(e, c0, c1):
-            codes, scales = w2q[e, 1]
             nc.vector.quantize_mx(
                 out=codes[:, c0:c1].bitcast(FP8X4),
                 scales=scales[:, c0:c1],
-                in_=pass1_columns(e, c0, c1).rearrange("p i t -> p (i t)"),
+                in_=columns(e, s, c0, c1).rearrange("p i t -> p (i t)"),
             )
 
         def quantize(values, width, tag):
-            codes = work.tile([P, width], U32, name=tag + "_codes", align_bytes=256)
-            scales = work.tile([P, width], U8, name=tag + "_scales", align_bytes=256)
-            nc.vector.quantize_mx(out=codes[:].bitcast(FP8X4), scales=scales[:], in_=values)
+            codes, scales = own_tile(tag + "_codes", [width], U32), own_tile(tag + "_scales", [width], U8)
+            nc.vector.quantize_mx(out=codes.bitcast(FP8X4), scales=scales, in_=values)
             return codes, scales
 
         def quantize_dh(e):
@@ -226,8 +201,8 @@ def tile_moe_dub_none_kernel(
         def quantize_w1(e):
             w1q[e] = quantize(grp1[e].rearrange("p k t -> p (k t)"), K, "w1")
 
-        def open_sums(e, c0, c1):
-            acc[e, c0] = psum.tile([P, c1 - c0], F32, name="acc")
+        def open_sums(e, c0, c1, name):
+            acc[e, c0] = psum.tile([P, c1 - c0], F32, name=name)
 
         def first_product(e, s, c0, c1):
             c = 0 if e * C < GATHER_CUTS[1] else 1
@@ -236,16 +211,34 @@ def tile_moe_dub_none_kernel(
             nc.tensor.matmul_mx(
                 out=acc[e, c0][:],
                 lhsT=g_words[s][c][:, slots].bitcast(FP8X4),
-                lhsT_scale=g_scales[c][SCALE_ROWS * s : P, slots],
+                lhsT_scale=g_scales[c][DY_SCALE_ROW + SCALE_ROWS * s : P, slots],
                 rhs=codes[:, c0:c1].bitcast(FP8X4),
                 rhs_scale=scales[:, c0:c1],
                 start=(s == 0),
                 stop=(s == PASSES - 1),
             )
 
-        def place_dh(e, first):
-            words = rounded[e][:, first : first + C, :].rearrange("p i t -> p (i t)").bitcast(F32)
-            return words.rearrange("j (u p) -> j u p", u=2)
+        def begin_pass1(e):
+            if e < FINE_FROM:
+                round_w2(e, 1, STEADY_CUT, H, nc.vector.tensor_copy)
+                round_w2(e, 1, 0, HALF_H)
+                round_w2(e, 1, HALF_H, STEADY_CUT)
+                quantize_w2(e, 1, 0, HALF_H)
+                return
+            round_w2(e, 1, 0, QUARTER_H, nc.vector.tensor_copy)
+            round_w2(e, 1, QUARTER_H, HALF_H, nc.vector.tensor_copy)
+            round_w2(e, 1, H - QUARTER_H, H)
+            round_w2(e, 1, HALF_H, H - QUARTER_H)
+            quantize_w2(e, 1, 0, QUARTER_H)
+            quantize_w2(e, 1, H - QUARTER_H, H)
+            if e == last:
+                first_product(e, 1, *LAST_PIECES[0])
+            quantize_w2(e, 1, QUARTER_H, HALF_H)
+            if e == last:
+                first_product(e, 1, *LAST_PIECES[1])
+
+        def finish_pass1(e):
+            quantize_w2(e, 1, HALF_H, H if e < FINE_FROM else H - QUARTER_H)
 
         def gate_sums(e, c0, c1):
             nc.scalar.activation(
@@ -280,15 +273,11 @@ def tile_moe_dub_none_kernel(
                     out=homes[h],
                     lhsT=codes,
                     lhsT_scale=scales,
-                    rhs=dq_codes[:].bitcast(FP8X4),
-                    rhs_scale=dq_scales[:],
+                    rhs=dq_codes.bitcast(FP8X4),
+                    rhs_scale=dq_scales,
                     start=True,
                     stop=True,
                 )
-
-        def own_bank(name):
-            fresh = psum.tile([P, 4, C], F32, name=name)
-            return fresh[:]
 
         def stage(source, home):
             nc.scalar.copy(out=home, in_=source)
@@ -305,80 +294,51 @@ def tile_moe_dub_none_kernel(
             for h in range(HALVES):
                 scatter(e, kind, h)
 
-        def own_tile(name, shape, dtype, bufs=WORK_BUFS):
-            fresh = work.tile([P] + shape, dtype, name=name, align_bytes=256, bufs=bufs)
-            return fresh[:]
-
-        def add_and_store(adder, queue, h, c0, c1):
-            total = work.tile([P, c1 - c0], F32, name="total", bufs=TOTAL_BUFS, align_bytes=256)
-            adder.tensor_tensor(total[:], dx_win[h][:, c0:c1], dp_win[h][:, c0:c1], ADD)
-            queue.dma_start(out=out[h * P : (h + 1) * P, c0:c1], in_=total[:])
-
-        def round_and_begin(e):
-            if e < FINE_FROM:
-                round_pass1(e, STEADY_CUT, H, nc.vector.tensor_copy)
-                round_pass1(e, 0, HALF_H, nc.scalar.copy)
-                round_pass1(e, HALF_H, STEADY_CUT, nc.scalar.copy)
-                quantize_pass1(e, 0, HALF_H)
-                return
-            round_pass1(e, 0, C, nc.vector.tensor_copy)
-            round_pass1(e, C, H - VECTOR_CUT, nc.vector.tensor_copy)
-            round_pass1(e, H - C, H, nc.scalar.copy)
-            if H - VECTOR_CUT < HALF_H:
-                round_pass1(e, H - VECTOR_CUT, HALF_H, nc.scalar.copy)
-            round_pass1(e, HALF_H, H - C, nc.scalar.copy)
-            quantize_pass1(e, 0, C)
-            quantize_pass1(e, H - C, H)
-            if e == E - 1:
-                first_product(e, 1, H - C, H)
-            quantize_pass1(e, C, HALF_H)
-            if e == E - 1:
-                first_product(e, 1, 0, HALF_H)
+        def add_and_store(adder, queue, h, c0, total):
+            c1 = c0 + total.shape[1]
+            adder.tensor_tensor(total, dx_win[h][:, c0:c1], dp_win[h][:, c0:c1], ADD)
+            queue.dma_start(out=out[h * P : (h + 1) * P, c0:c1], in_=total)
 
         gather_words(0, 0)
         gather_scales(0)
         gather_words(0, 1)
         gather_words(1, 0)
         gather_words(1, 1)
-        open_expert(0)
-        grp2[0, 0, 1] = own_tile("first_high", [HALF_H, PACK], BF16, 1)
+        open_expert(0, own_tile("first_high", [HALF_H, PACK], BF16, 1))
         round_w2(0, 0, 0, HALF_H)
         round_w2(0, 0, HALF_H, H)
-        quantize_w2(0, 0, 0)
-        quantize_w2(0, 0, 1)
-        open_sums(0, 0, H)
+        quantize_w2(0, 0, 0, HALF_H)
+        quantize_w2(0, 0, HALF_H, H)
+        open_sums(0, 0, H, "acc")
         first_product(0, 0, 0, H)
-        round_and_begin(0)
+        begin_pass1(0)
         gate_t = own_bank("turned")
         nc.tensor.transpose(gate_t[:, 0, :], gate_rows[:], ident[:])
         nc.scalar.activation(out=gate_cols[:], in_=gate_t[:, 0, 0:E], func=COPY)
+        bank[0] = own_bank("turned")
 
-        last = E - 1
         for e in range(last):
             nxt, prev = e + 1, e - 1
-            quantize_pass1(e, HALF_H, H if e < FINE_FROM else H - C)
+            finish_pass1(e)
             first_product(e, 1, 0, H)
-            open_expert(nxt)
-            grp2[nxt, 0, 1] = grp2[e, 1, 1] if e else second_high[:]
-            grp1[e] = grp2[e, 1, 0]
+            open_expert(nxt, spent[e][:, HALF_H:H, :])
+            grp1[e] = spent[e][:, 0:HALF_H, :]
             if e == 0:
                 gather_scales(1)
                 round_w2(nxt, 0, GPSIMD_CUT, H, nc.vector.tensor_copy)
                 interleave(nc.vector.tensor_copy, grp1[e], raw1[e][:])
             else:
-                round_w2_on_gpsimd(nxt, 0, GPSIMD_CUT, H)
+                round_on_gpsimd(columns(nxt, 0, GPSIMD_CUT, H), raw2[nxt, 0][:, :, GPSIMD_CUT:H])
                 round_on_gpsimd(grp1[e], raw1[e][:])
                 scatters(prev, "p")
                 scatters(prev, "x")
-            round_w2(nxt, 0, 0, FIRST_CUT)
-            round_w2(nxt, 0, FIRST_CUT, 2 * FIRST_CUT)
-            if e == 0:
-                bank[e] = own_bank("turned")
-            dh[e] = flat2[nxt, 0][:, DH_START : DH_START + 2 * C].rearrange("j (u p) -> j u p", u=2)
+            round_w2(nxt, 0, 0, FIRST_PIECE)
+            round_w2(nxt, 0, FIRST_PIECE, 2 * FIRST_PIECE)
+            dh[e] = w2_tile[nxt, 0][:, DH_START : DH_START + 2 * C].rearrange("j (u p) -> j u p", u=2)
             gate_sums(e, 0, H)
             turn(e)
             round_w2(nxt, 0, HALF_H, GPSIMD_CUT)
-            round_w2(nxt, 0, 2 * FIRST_CUT, HALF_H - HELD_COLUMNS)
+            round_w2(nxt, 0, 2 * FIRST_PIECE, HALF_H - HELD_COLUMNS)
             copy_turned(e)
             round_w2(nxt, 0, HALF_H - HELD_COLUMNS, HALF_H)
             quantize_dh(e)
@@ -388,21 +348,22 @@ def tile_moe_dub_none_kernel(
             second_product(e, "p", [sums_p[:, h, :] for h in range(HALVES)])
             before_last = nxt == last
             second_product(e, "x", [sums_x[:, 0, :], bank[nxt][:, 2, :] if before_last else sums_x[:, 1, :]])
-            quantize_w2(nxt, 0, 1)
-            quantize_w2(nxt, 0, 0)
+            quantize_w2(nxt, 0, HALF_H, H)
+            quantize_w2(nxt, 0, 0, HALF_H)
             if before_last:
-                for c0, c1 in PIECES:
-                    acc[nxt, c0] = psum.tile([P, c1 - c0], F32, name="acc" if c0 < H - C else "sums_x")
-                for c0, c1 in PIECES:
+                for (c0, c1), name in zip(LAST_PIECES, ("sums_x", "acc", "acc")):
+                    open_sums(nxt, c0, c1, name)
+                for c0, c1 in LAST_PIECES:
                     first_product(nxt, 0, c0, c1)
             else:
-                open_sums(nxt, 0, H)
+                open_sums(nxt, 0, H, "acc")
                 first_product(nxt, 0, 0, H)
-            round_and_begin(nxt)
-            homes = raw2[nxt, 1][:, :, 0:C] if nxt < FINE_FROM else raw2[nxt, 1][:, :, H - C : H]
+            begin_pass1(nxt)
             if nxt < FINE_FROM:
+                homes = raw2[nxt, 1][:, :, 0:C]
                 stage(sums_p[:, 0:HALVES, :], homes[:, 0:HALVES, :])
             else:
+                homes = raw2[nxt, 1][:, :, H - C : H]
                 for h in range(HALVES):
                     stage(sums_p[:, h, :], homes[:, h, :])
             ready = 1 if before_last else HALVES
@@ -412,19 +373,20 @@ def tile_moe_dub_none_kernel(
 
         prev = last - 1
         w1_cut = K - HELD_W1_COLUMNS
-        quantize_pass1(last, *PIECES[2])
-        first_product(last, 1, *PIECES[2])
-        grp1[last] = grp2[last, 1, 1]
+        finish_pass1(last)
+        first_product(last, 1, *LAST_PIECES[2])
+        grp1[last] = spent[last][:, HALF_H:H, :]
         round_on_gpsimd(grp1[last][:, 0:w1_cut, :], raw1[last][:, :, 0:w1_cut])
         scatters(prev, "p")
         scatter(prev, "x", 0)
-        dh[last] = place_dh(last, PASS1_START + H - HELD_W1_COLUMNS)
-        for c0, c1 in PIECES:
+        dh_columns = spent[last][:, H - HELD_W1_COLUMNS : H - HELD_W1_COLUMNS + C, :]
+        dh[last] = dh_columns.rearrange("p i t -> p (i t)").bitcast(F32).rearrange("j (u p) -> j u p", u=2)
+        for c0, c1 in LAST_PIECES:
             gate_sums(last, c0, c1)
         turn(last)
         copy_turned(last)
         interleave(nc.scalar.copy, grp1[last][:, w1_cut:K, :], raw1[last][:, :, w1_cut:K])
-        staged[prev, "x", 1] = own_tile("staged", [C], F32)
+        staged[prev, "x", 1] = raw1[last][:, 0, 0:C]
         stage(bank[last][:, 2, :], staged[prev, "x", 1])
         quantize_dh(last)
         quantize_w1(last)
@@ -433,17 +395,17 @@ def tile_moe_dub_none_kernel(
         second_product(last, "p", last_sums["p"])
         second_product(last, "x", last_sums["x"])
         scatter(prev, "x", 1)
+        late_totals = {kind: own_tile("total", [T // 4], F32, TOTAL_BUFS) for kind in "px"}
         for h in range(HALVES):
             for kind in "px":
-                staged[last, kind, h] = own_tile("staged", [C], F32)
+                staged[last, kind, h] = late_totals[kind][:, 0:C] if h else own_tile("staged", [C], F32)
                 stage(last_sums[kind][h], staged[last, kind, h])
         for h in range(HALVES):
             scatter(last, "p", h)
             scatter(last, "x", h)
 
-        add_and_store(nc.gpsimd, nc.scalar, 0, 0, GPSIMD_ADD)
-        add_and_store(nc.gpsimd, nc.scalar, 0, GPSIMD_ADD, 2 * GPSIMD_ADD)
-        add_and_store(nc.vector, nc.sync, 0, 2 * GPSIMD_ADD, 3 * GPSIMD_ADD)
-        add_and_store(nc.vector, nc.sync, 0, 3 * GPSIMD_ADD, T)
-        for c0, c1 in zip(ADD_CUTS, ADD_CUTS[1:]):
-            add_and_store(nc.vector, nc.sync, 1, c0, c1)
+        add_and_store(nc.gpsimd, nc.scalar, 0, 0, own_tile("total", [T // 2], F32, TOTAL_BUFS))
+        add_and_store(nc.vector, nc.sync, 0, T // 2, late_totals["p"])
+        add_and_store(nc.vector, nc.sync, 0, 3 * T // 4, late_totals["x"])
+        for c0 in (0, T // 2):
+            add_and_store(nc.vector, nc.sync, 1, c0, own_tile("total", [T // 2], F32, TOTAL_BUFS))

@@ -28,6 +28,7 @@ SCALE_ROWS = 4
 DY_SCALE_ROW = 8
 LIST_STEP = 16
 ALIGN = 256
+ROW_ALIGN = 1024
 HALF_H = H // 2
 QUARTER_H = H // 4
 GATHER_CUTS = (0, 2 * C, E * C)
@@ -37,8 +38,9 @@ LAST_PIECES = ((H - QUARTER_H, H), (0, HALF_H), (HALF_H, H - QUARTER_H))
 GPSIMD_CUT = 352
 FIRST_PIECE = 64
 HELD_COLUMNS = 32
-DH_START = 2 * (HALF_H - HELD_COLUMNS)
-FRONT = DH_START + 2 * C - FIRST_PIECE
+FRONT = 3 * ROW_ALIGN // 4
+DH_START = FRONT + FIRST_PIECE - 2 * C
+LOW_START = DH_START - 2 * (HALF_H - HELD_COLUMNS)
 HELD_W1_COLUMNS = 32
 RAW_W2_BUFS = 5
 ROUNDED_BUFS = 3
@@ -69,8 +71,8 @@ def tile_moe_dub_none_kernel(
         piece_widths = [b - a for a, b in zip(GATHER_CUTS, GATHER_CUTS[1:])]
         token_list = keep.tile([P, T // LIST_STEP], U16, name="token_list", align_bytes=ALIGN)
         partner_list = keep.tile([P, T // LIST_STEP], U16, name="partner_list", align_bytes=ALIGN)
-        dy_win = [keep.tile([P, T], I32, name="dy_win%d" % s, align_bytes=ALIGN) for s in range(PASSES)]
-        dys_win = keep.tile([P, T], U8, name="dys_win", align_bytes=ALIGN)
+        dy_win = [keep.tile([P, T], I32, name="dy_win%d" % s, align_bytes=ROW_ALIGN) for s in range(PASSES)]
+        dys_win = keep.tile([P, T], U8, name="dys_win", align_bytes=ROW_ALIGN)
         g_words = [
             [keep.tile([P, w], U32, name="g_words%d_%d" % (s, c), align_bytes=ALIGN) for c, w in enumerate(piece_widths)]
             for s in range(PASSES)
@@ -80,7 +82,7 @@ def tile_moe_dub_none_kernel(
             keep.tile([P, piece_widths[0]], U8, name="g_scales0", align_bytes=ALIGN),
             head.tile([P, piece_widths[1]], U8, name="g_scales1", align_bytes=ALIGN, offset=0),
         ]
-        wp_words = keep.tile([P, E, 2 * K], U8, name="wp_words", align_bytes=ALIGN)
+        wp_words = keep.tile([P, E, 2 * K], U8, name="wp_words", align_bytes=ROW_ALIGN)
         wp_scales = keep.tile([P, E, K], U8, name="wp_scales", align_bytes=ALIGN)
         gate_rows = keep.tile([P, C], F32, name="gate_rows", align_bytes=ALIGN)
         gate_cols = keep.tile([P, E], F32, name="gate_cols")
@@ -103,13 +105,13 @@ def tile_moe_dub_none_kernel(
 
         def load_w2(e, s):
             front = FRONT if s == 0 else 0
-            w2_tile[e, s] = raw2_pool.tile([P, front + PACK * H], F32, name="raw2_pass%d" % s, align_bytes=ALIGN)
+            w2_tile[e, s] = raw2_pool.tile([P, front + PACK * H], F32, name="raw2_pass%d" % s, align_bytes=ROW_ALIGN)
             raw2[e, s] = w2_tile[e, s][:, front:].rearrange("p (j i) -> p j i", j=PACK)
             rows = w2t[e, s * PASS : (s + 1) * PASS, :]
             nc.sync.dma_start(out=w2_tile[e, s][:, front:], in_=rows.rearrange("(p j) i -> p (j i)", j=PACK))
 
         def load_w1(e):
-            raw1[e] = raw1_pool.tile([P, PACK, K], F32, name="raw1", align_bytes=ALIGN)
+            raw1[e] = raw1_pool.tile([P, PACK, K], F32, name="raw1", align_bytes=ROW_ALIGN)
             nc.sync.dma_start(
                 out=raw1[e][:].rearrange("p j k -> p (j k)"), in_=w1t[e].rearrange("(p j) k -> p (j k)", j=PACK)
             )
@@ -149,6 +151,10 @@ def tile_moe_dub_none_kernel(
             fresh = work.tile([P] + shape, dtype, name=name, align_bytes=ALIGN, bufs=bufs)
             return fresh[:]
 
+        def total_tile(width):
+            fresh = work.tile([P, width], F32, name="total", align_bytes=ROW_ALIGN, bufs=TOTAL_BUFS)
+            return fresh[:]
+
         def own_bank(name):
             fresh = psum.tile([P, 4, C], F32, name=name)
             return fresh[:]
@@ -164,7 +170,7 @@ def tile_moe_dub_none_kernel(
 
         def open_expert(e, high_home):
             spent[e] = own_tile("rounded", [H + C - HELD_W1_COLUMNS, PACK], BF16, ROUNDED_BUFS)
-            low_home = w2_tile[e, 0][:, 0:H].bitcast(BF16).rearrange("p (i t) -> p i t", t=PACK)
+            low_home = w2_tile[e, 0][:, LOW_START : LOW_START + H].bitcast(BF16).rearrange("p (i t) -> p i t", t=PACK)
             pass0[e] = low_home, high_home
             pass1[e] = spent[e][:, 0:H, :] if e else first_pass1[:]
             for s in range(PASSES):
@@ -395,7 +401,7 @@ def tile_moe_dub_none_kernel(
         second_product(last, "p", last_sums["p"])
         second_product(last, "x", last_sums["x"])
         scatter(prev, "x", 1)
-        late_totals = {kind: own_tile("total", [T // 4], F32, TOTAL_BUFS) for kind in "px"}
+        late_totals = {kind: total_tile(T // 4) for kind in "px"}
         for h in range(HALVES):
             for kind in "px":
                 staged[last, kind, h] = late_totals[kind][:, 0:C] if h else own_tile("staged", [C], F32)
@@ -404,8 +410,8 @@ def tile_moe_dub_none_kernel(
             scatter(last, "p", h)
             scatter(last, "x", h)
 
-        add_and_store(nc.gpsimd, nc.scalar, 0, 0, own_tile("total", [T // 2], F32, TOTAL_BUFS))
+        add_and_store(nc.gpsimd, nc.scalar, 0, 0, total_tile(T // 2))
         add_and_store(nc.vector, nc.sync, 0, T // 2, late_totals["p"])
         add_and_store(nc.vector, nc.sync, 0, 3 * T // 4, late_totals["x"])
         for c0 in (0, T // 2):
-            add_and_store(nc.vector, nc.sync, 1, c0, own_tile("total", [T // 2], F32, TOTAL_BUFS))
+            add_and_store(nc.vector, nc.sync, 1, c0, total_tile(T // 2))

from contextlib import ExitStack

import concourse.mybir as mybir
from concourse.masks import make_identity

K, T, E, C, H, N = 256, 1024, 8, 128, 512, 1024
FLOPS = 2 * E * C * (N * H + 2 * H * K)

F32 = mybir.dt.float32
BF16 = mybir.dt.bfloat16
I32 = mybir.dt.int32
U32 = mybir.dt.uint32
U16 = mybir.dt.uint16
U8 = mybir.dt.uint8
FP8X4 = mybir.dt.float8_e4m3fn_x4
FP4X4 = mybir.dt.float4_e2m1fn_x4
COPY = mybir.ActivationFunctionType.Copy
ADD = mybir.AluOpType.add
MULT = mybir.AluOpType.mult

P = 128
PACK = 4
PASS = P * PACK
PASSES = N // PASS
HALVES = K // P
QUADRANTS = 4
SCALE_ROWS = 4
DY_SCALE_ROW = 8
LIST_STEP = 16
ALIGN = 256
ROW_ALIGN = 1024
HALF_H = H // 2
QUARTER_H = H // 4
GATHER_CUTS = (0, 2 * C, E * C)
STEADY_CUT = 336
FINE_FROM = 5
LAST_PIECES = ((H - QUARTER_H, H), (0, HALF_H), (HALF_H, H - QUARTER_H))
GPSIMD_CUT = 352
FIRST_PIECE = 64
HELD_COLUMNS = 32
FRONT = 3 * ROW_ALIGN // 4
DH_START = FRONT + FIRST_PIECE - 2 * C
LOW_START = DH_START - 2 * (HALF_H - HELD_COLUMNS)
HELD_W1_COLUMNS = 32
RAW_W2_BUFS = 5
ROUNDED_BUFS = 3
WORK_BUFS = 4
TOTAL_BUFS = 5


def interleave(copy, grouped, raw):
    copy(
        out=grouped.rearrange("p (c i) t -> p c t i", i=2),
        in_=raw.rearrange("p t (c i) -> p c t i", i=2),
    )


def tile_moe_dub_none_kernel(
    tc, dy_words, dy_scales, w2t, w1t, wpt_words, wpt_scales, gate, offs, offs2, out
):
    nc = tc.nc
    last = E - 1
    with ExitStack() as ctx:
        keep = ctx.enter_context(tc.tile_pool(name="keep", bufs=1))
        raw2_pool = ctx.enter_context(tc.tile_pool(name="raw2", bufs=RAW_W2_BUFS))
        raw1_pool = ctx.enter_context(tc.tile_pool(name="raw1", bufs=E))
        work = ctx.enter_context(tc.tile_pool(name="work", bufs=WORK_BUFS))
        head = ctx.enter_context(tc.tile_pool(name="head", bufs=1))
        psum = ctx.enter_context(tc.psum_pool(name="psum", bufs=2))

        piece_widths = [b - a for a, b in zip(GATHER_CUTS, GATHER_CUTS[1:])]
        token_list = keep.tile([P, T // LIST_STEP], U16, name="token_list", align_bytes=ALIGN)
        partner_list = keep.tile([P, T // LIST_STEP], U16, name="partner_list", align_bytes=ALIGN)
        dy_win = [keep.tile([P, T], I32, name="dy_win%d" % s, align_bytes=ROW_ALIGN) for s in range(PASSES)]
        dys_win = keep.tile([P, T], U8, name="dys_win", align_bytes=ROW_ALIGN)
        g_words = [
            [keep.tile([P, w], U32, name="g_words%d_%d" % (s, c), align_bytes=ALIGN) for c, w in enumerate(piece_widths)]
            for s in range(PASSES)
        ]
        first_pass1 = head.tile([P, H, PACK], BF16, name="first_pass1", align_bytes=ALIGN, offset=0)
        g_scales = [
            keep.tile([P, piece_widths[0]], U8, name="g_scales0", align_bytes=ALIGN),
            head.tile([P, piece_widths[1]], U8, name="g_scales1", align_bytes=ALIGN, offset=0),
        ]
        wp_words = keep.tile([P, E, 2 * K], U8, name="wp_words", align_bytes=ROW_ALIGN)
        wp_scales = keep.tile([P, E, K], U8, name="wp_scales", align_bytes=ALIGN)
        gate_rows = keep.tile([P, C], F32, name="gate_rows", align_bytes=ALIGN)
        gate_cols = keep.tile([P, E], F32, name="gate_cols")
        ident = keep.tile([P, P], F32, name="ident")
        dx_win = [keep.tile([P, T], F32, name="dx_win%d" % h) for h in range(HALVES)]
        dp_win = [keep.tile([P, T], F32, name="dp_win%d" % h) for h in range(HALVES)]

        nc.vector.memset(dys_win[:].bitcast(I32), 0)
        make_identity(nc, ident[:])
        nc.gpsimd.memset(gate_rows[:], 0.0)
        nc.gpsimd.memset(wp_scales[:].rearrange("p e k -> p (e k)").bitcast(I32), 0)
        for r in range(SCALE_ROWS):
            nc.gpsimd.dma_start(
                out=wp_scales[r:P:32, :, :].bitcast(I32),
                in_=wpt_scales[:, 0, r : QUADRANTS * SCALE_ROWS : SCALE_ROWS, :].rearrange("e q k -> q e k").bitcast(I32),
            )

        w2_tile, raw2, raw1, spent, pass0, pass1, grp1 = [{} for n in range(7)]
        w2q, w1q, acc, dh, bank, dh_t, dq, staged = [{} for n in range(8)]

        def load_w2(e, s):
            front = FRONT if s == 0 else 0
            w2_tile[e, s] = raw2_pool.tile([P, front + PACK * H], F32, name="raw2_pass%d" % s, align_bytes=ROW_ALIGN)
            raw2[e, s] = w2_tile[e, s][:, front:].rearrange("p (j i) -> p j i", j=PACK)
            rows = w2t[e, s * PASS : (s + 1) * PASS, :]
            nc.sync.dma_start(out=w2_tile[e, s][:, front:], in_=rows.rearrange("(p j) i -> p (j i)", j=PACK))

        def load_w1(e):
            raw1[e] = raw1_pool.tile([P, PACK, K], F32, name="raw1", align_bytes=ROW_ALIGN)
            nc.sync.dma_start(
                out=raw1[e][:].rearrange("p j k -> p (j k)"), in_=w1t[e].rearrange("(p j) k -> p (j k)", j=PACK)
            )

        def load_dy(s):
            nc.sync.dma_start(out=dy_win[s][:], in_=dy_words[s].rearrange("p t d -> p (t d)").bitcast(I32))

        def load_dy_scales(s):
            for r in range(SCALE_ROWS):
                nc.sync.dma_start(
                    out=dys_win[DY_SCALE_ROW + SCALE_ROWS * s + r : P : 32, :].bitcast(I32),
                    in_=dy_scales[s, r : QUADRANTS * SCALE_ROWS : SCALE_ROWS, :].bitcast(I32),
                )

        def load_wp(e):
            nc.sync.dma_start(out=wp_words[:, e, :].bitcast(I32), in_=wpt_words[e, 0].bitcast(I32))

        nc.sync.dma_start(token_list[:], offs)
        load_dy(0)
        load_dy(1)
        load_dy_scales(0)
        load_w2(0, 0)
        load_dy_scales(1)
        load_w2(0, 1)
        nc.sync.dma_start(out=gate_rows[0:E, :], in_=gate.rearrange("p (e u) -> (p e) u", u=C)[0:E, :])
        for e in range(1, E):
            load_w2(e, 0)
            if e == 1:
                nc.sync.dma_start(partner_list[:], offs2)
            load_w1(e - 1)
            load_wp(e - 1)
            load_w2(e, 1)
        load_w1(last)
        load_wp(last)

        def own_tile(name, shape, dtype, bufs=WORK_BUFS):
            fresh = work.tile([P] + shape, dtype, name=name, align_bytes=ALIGN, bufs=bufs)
            return fresh[:]

        def total_tile(width):
            fresh = work.tile([P, width], F32, name="total", align_bytes=ROW_ALIGN, bufs=TOTAL_BUFS)
            return fresh[:]

        def own_bank(name):
            fresh = psum.tile([P, 4, C], F32, name=name)
            return fresh[:]

        def picks(c):
            return token_list[:, GATHER_CUTS[c] // LIST_STEP : GATHER_CUTS[c + 1] // LIST_STEP]

        def gather_words(s, c):
            nc.vector.tensor_copy(g_words[s][c][:], dy_win[s][:].bitcast(U32).indirect(picks(c)))

        def gather_scales(c):
            nc.vector.tensor_copy(g_scales[c][:], dys_win[:].indirect(picks(c)))

        def open_expert(e, high_home):
            spent[e] = own_tile("rounded", [H + C - HELD_W1_COLUMNS, PACK], BF16, ROUNDED_BUFS)
            low_home = w2_tile[e, 0][:, LOW_START : LOW_START + H].bitcast(BF16).rearrange("p (i t) -> p i t", t=PACK)
            pass0[e] = low_home, high_home
            pass1[e] = spent[e][:, 0:H, :] if e else first_pass1[:]
            for s in range(PASSES):
                w2q[e, s] = own_tile("w2_codes", [H], U32), own_tile("w2_scales", [H], U8)

        def columns(e, s, c0, c1):
            if s == 1:
                return pass1[e][:, c0:c1, :]
            half = c0 // HALF_H
            return pass0[e][half][:, c0 - half * HALF_H : c1 - half * HALF_H, :]

        def round_w2(e, s, c0, c1, copy=nc.scalar.copy):
            interleave(copy, columns(e, s, c0, c1), raw2[e, s][:, :, c0:c1])

        def round_on_gpsimd(grouped, raw):
            nc.gpsimd.tensor_scalar(grouped, raw.rearrange("p t c -> p c t"), 1.0, 0.0, MULT, ADD)

        def quantize_w2(e, s, c0, c1):
            codes, scales = w2q[e, s]
            nc.vector.quantize_mx(
                out=codes[:, c0:c1].bitcast(FP8X4),
                scales=scales[:, c0:c1],
                in_=columns(e, s, c0, c1).rearrange("p i t -> p (i t)"),
            )

        def quantize(values, width, tag):
            codes, scales = own_tile(tag + "_codes", [width], U32), own_tile(tag + "_scales", [width], U8)
            nc.vector.quantize_mx(out=codes.bitcast(FP8X4), scales=scales, in_=values)
            return codes, scales

        def quantize_dh(e):
            dq[e] = quantize(dh_t[e], C, "dh")

        def quantize_w1(e):
            w1q[e] = quantize(grp1[e].rearrange("p k t -> p (k t)"), K, "w1")

        def open_sums(e, c0, c1, name):
            acc[e, c0] = psum.tile([P, c1 - c0], F32, name=name)

        def first_product(e, s, c0, c1):
            c = 0 if e * C < GATHER_CUTS[1] else 1
            slots = slice(e * C - GATHER_CUTS[c], (e + 1) * C - GATHER_CUTS[c])
            codes, scales = w2q[e, s]
            nc.tensor.matmul_mx(
                out=acc[e, c0][:],
                lhsT=g_words[s][c][:, slots].bitcast(FP8X4),
                lhsT_scale=g_scales[c][DY_SCALE_ROW + SCALE_ROWS * s : P, slots],
                rhs=codes[:, c0:c1].bitcast(FP8X4),
                rhs_scale=scales[:, c0:c1],
                start=(s == 0),
                stop=(s == PASSES - 1),
            )

        def begin_pass1(e):
            if e < FINE_FROM:
                round_w2(e, 1, STEADY_CUT, H, nc.vector.tensor_copy)
                round_w2(e, 1, 0, HALF_H)
                round_w2(e, 1, HALF_H, STEADY_CUT)
                quantize_w2(e, 1, 0, HALF_H)
                return
            round_w2(e, 1, 0, QUARTER_H, nc.vector.tensor_copy)
            round_w2(e, 1, QUARTER_H, HALF_H, nc.vector.tensor_copy)
            round_w2(e, 1, H - QUARTER_H, H)
            round_w2(e, 1, HALF_H, H - QUARTER_H)
            quantize_w2(e, 1, 0, QUARTER_H)
            quantize_w2(e, 1, H - QUARTER_H, H)
            if e == last:
                first_product(e, 1, *LAST_PIECES[0])
            quantize_w2(e, 1, QUARTER_H, HALF_H)
            if e == last:
                first_product(e, 1, *LAST_PIECES[1])

        def finish_pass1(e):
            quantize_w2(e, 1, HALF_H, H if e < FINE_FROM else H - QUARTER_H)

        def gate_sums(e, c0, c1):
            nc.scalar.activation(
                out=dh[e][:, :, c0 // PACK : c1 // PACK].bitcast(BF16).rearrange("j u (p d) -> j u p d", d=2),
                in_=acc[e, c0][:].rearrange("j (p u d) -> j u p d", u=2, d=2),
                func=COPY,
                scale=gate_cols[:, e : e + 1],
            )

        def turn(e):
            for u in (1, 0):
                nc.tensor.transpose(bank[e][:, u, :], dh[e][:, u, :], ident[:])

        def copy_turned(e):
            dh_t[e] = own_tile("dh_t", [H], BF16)
            nc.scalar.copy(
                out=dh_t[e].bitcast(F32).rearrange("p (j u) -> p j u", u=2),
                in_=bank[e][:, 0:2, :].rearrange("p u j -> p j u"),
            )

        def second_product(e, kind, homes):
            dq_codes, dq_scales = dq[e]
            for h in range(HALVES):
                cols = slice(P * h, P * (h + 1))
                if kind == "p":
                    codes = wp_words[:, e, 2 * P * h : 2 * P * (h + 1)].bitcast(FP4X4)
                    scales = wp_scales[:, e, cols]
                else:
                    codes = w1q[e][0][:, cols].bitcast(FP8X4)
                    scales = w1q[e][1][:, cols]
                nc.tensor.matmul_mx(
                    out=homes[h],
                    lhsT=codes,
                    lhsT_scale=scales,
                    rhs=dq_codes.bitcast(FP8X4),
                    rhs_scale=dq_scales,
                    start=True,
                    stop=True,
                )

        def stage(source, home):
            nc.scalar.copy(out=home, in_=source)

        def scatter(e, kind, h):
            cols = slice(e * C // LIST_STEP, (e + 1) * C // LIST_STEP)
            if kind == "p":
                window = dp_win[h][:].indirect(partner_list[:, cols])
            else:
                window = dx_win[h][:].indirect(token_list[:, cols])
            nc.vector.tensor_copy(window, staged[e, kind, h])

        def scatters(e, kind):
            for h in range(HALVES):
                scatter(e, kind, h)

        def add_and_store(adder, queue, h, c0, total):
            c1 = c0 + total.shape[1]
            adder.tensor_tensor(total, dx_win[h][:, c0:c1], dp_win[h][:, c0:c1], ADD)
            queue.dma_start(out=out[h * P : (h + 1) * P, c0:c1], in_=total)

        gather_words(0, 0)
        gather_scales(0)
        gather_words(0, 1)
        gather_words(1, 0)
        gather_words(1, 1)
        open_expert(0, own_tile("first_high", [HALF_H, PACK], BF16, 1))
        round_w2(0, 0, 0, HALF_H)
        round_w2(0, 0, HALF_H, H)
        quantize_w2(0, 0, 0, HALF_H)
        quantize_w2(0, 0, HALF_H, H)
        open_sums(0, 0, H, "acc")
        first_product(0, 0, 0, H)
        begin_pass1(0)
        gate_t = own_bank("turned")
        nc.tensor.transpose(gate_t[:, 0, :], gate_rows[:], ident[:])
        nc.scalar.activation(out=gate_cols[:], in_=gate_t[:, 0, 0:E], func=COPY)
        bank[0] = own_bank("turned")

        for e in range(last):
            nxt, prev = e + 1, e - 1
            finish_pass1(e)
            first_product(e, 1, 0, H)
            open_expert(nxt, spent[e][:, HALF_H:H, :])
            grp1[e] = spent[e][:, 0:HALF_H, :]
            if e == 0:
                gather_scales(1)
                round_w2(nxt, 0, GPSIMD_CUT, H, nc.vector.tensor_copy)
                interleave(nc.vector.tensor_copy, grp1[e], raw1[e][:])
            else:
                round_on_gpsimd(columns(nxt, 0, GPSIMD_CUT, H), raw2[nxt, 0][:, :, GPSIMD_CUT:H])
                round_on_gpsimd(grp1[e], raw1[e][:])
                scatters(prev, "p")
                scatters(prev, "x")
            round_w2(nxt, 0, 0, FIRST_PIECE)
            round_w2(nxt, 0, FIRST_PIECE, 2 * FIRST_PIECE)
            dh[e] = w2_tile[nxt, 0][:, DH_START : DH_START + 2 * C].rearrange("j (u p) -> j u p", u=2)
            gate_sums(e, 0, H)
            turn(e)
            round_w2(nxt, 0, HALF_H, GPSIMD_CUT)
            round_w2(nxt, 0, 2 * FIRST_PIECE, HALF_H - HELD_COLUMNS)
            copy_turned(e)
            round_w2(nxt, 0, HALF_H - HELD_COLUMNS, HALF_H)
            quantize_dh(e)
            quantize_w1(e)
            bank[nxt] = own_bank("turned")
            sums_p, sums_x = own_bank("sums_p"), own_bank("sums_x")
            second_product(e, "p", [sums_p[:, h, :] for h in range(HALVES)])
            before_last = nxt == last
            second_product(e, "x", [sums_x[:, 0, :], bank[nxt][:, 2, :] if before_last else sums_x[:, 1, :]])
            quantize_w2(nxt, 0, HALF_H, H)
            quantize_w2(nxt, 0, 0, HALF_H)
            if before_last:
                for (c0, c1), name in zip(LAST_PIECES, ("sums_x", "acc", "acc")):
                    open_sums(nxt, c0, c1, name)
                for c0, c1 in LAST_PIECES:
                    first_product(nxt, 0, c0, c1)
            else:
                open_sums(nxt, 0, H, "acc")
                first_product(nxt, 0, 0, H)
            begin_pass1(nxt)
            if nxt < FINE_FROM:
                homes = raw2[nxt, 1][:, :, 0:C]
                stage(sums_p[:, 0:HALVES, :], homes[:, 0:HALVES, :])
            else:
                homes = raw2[nxt, 1][:, :, H - C : H]
                for h in range(HALVES):
                    stage(sums_p[:, h, :], homes[:, h, :])
            ready = 1 if before_last else HALVES
            stage(sums_x[:, 0:ready, :], homes[:, HALVES : HALVES + ready, :])
            for h in range(HALVES):
                staged[e, "p", h], staged[e, "x", h] = homes[:, h, :], homes[:, HALVES + h, :]

        prev = last - 1
        w1_cut = K - HELD_W1_COLUMNS
        finish_pass1(last)
        first_product(last, 1, *LAST_PIECES[2])
        grp1[last] = spent[last][:, HALF_H:H, :]
        round_on_gpsimd(grp1[last][:, 0:w1_cut, :], raw1[last][:, :, 0:w1_cut])
        scatters(prev, "p")
        scatter(prev, "x", 0)
        dh_columns = spent[last][:, H - HELD_W1_COLUMNS : H - HELD_W1_COLUMNS + C, :]
        dh[last] = dh_columns.rearrange("p i t -> p (i t)").bitcast(F32).rearrange("j (u p) -> j u p", u=2)
        for c0, c1 in LAST_PIECES:
            gate_sums(last, c0, c1)
        turn(last)
        copy_turned(last)
        interleave(nc.scalar.copy, grp1[last][:, w1_cut:K, :], raw1[last][:, :, w1_cut:K])
        staged[prev, "x", 1] = raw1[last][:, 0, 0:C]
        stage(bank[last][:, 2, :], staged[prev, "x", 1])
        quantize_dh(last)
        quantize_w1(last)
        first, middle, final = own_bank("sums_p"), own_bank("sums_x"), own_bank("sums_p")
        last_sums = {"p": [first[:, 0, :], final[:, 0, :]], "x": [middle[:, 0, :], final[:, 1, :]]}
        second_product(last, "p", last_sums["p"])
        second_product(last, "x", last_sums["x"])
        scatter(prev, "x", 1)
        late_totals = {kind: total_tile(T // 4) for kind in "px"}
        for h in range(HALVES):
            for kind in "px":
                staged[last, kind, h] = late_totals[kind][:, 0:C] if h else own_tile("staged", [C], F32)
                stage(last_sums[kind][h], staged[last, kind, h])
        for h in range(HALVES):
            scatter(last, "p", h)
            scatter(last, "x", h)

        add_and_store(nc.gpsimd, nc.scalar, 0, 0, total_tile(T // 2))
        add_and_store(nc.vector, nc.sync, 0, T // 2, late_totals["p"])
        add_and_store(nc.vector, nc.sync, 0, 3 * T // 4, late_totals["x"])
        for c0 in (0, T // 2):
            add_and_store(nc.vector, nc.sync, 1, c0, total_tile(T // 2))
